import numpy as np, ml_dtypes
CORES = [5,29,101,125,133,157,229,253]
N = 8
import mx_ref
BF = ml_dtypes.bfloat16
def entries(a):
    return np.ascontiguousarray(a.T).reshape(-1)
def table(e):
    return np.ascontiguousarray(np.reshape(e, (-1, 16)).T).astype(np.int32)
def cols(t, e):
    v = np.concatenate([t.reshape(128, -1, 4), np.zeros((128, 1, 4), BF)], axis=1)
    return np.ascontiguousarray(v[:, e]).reshape(128, -1)
def cut(t, i, w=512):
    return t[:, w * i:w * i + w]
def pick(q, e):
    c = np.concatenate([q[0].reshape(128, -1, 4), np.zeros((128, 1, 4), np.uint8)], axis=1); s = np.concatenate([q[1], np.ones((16, 1), np.uint8)], axis=1)
    return (np.ascontiguousarray(c[:, e].reshape(128, -1)), np.ascontiguousarray(s[:, e]))
def join(*qs):
    return (np.concatenate([q[0] for q in qs], axis=1), np.concatenate([q[1] for q in qs], axis=1))
def put(q, e, v):
    c, s = q[0].reshape(128, -1, 4).copy(), q[1].copy(); c[:, e] = v[0].reshape(128, -1, 4); s[:, e] = v[1]
    return (c.reshape(128, -1), s)
def pk(c, s):
    return (np.ascontiguousarray(c), mx_ref.live(s))
def emit(q):
    return q[0], q[1]
def decode(q):
    o = []
    for b in range(4):
        e = np.zeros((128, 128, 4), np.float32); e[np.arange(128), np.arange(128), b] = 1
        o.append(mx_ref.matmul(mx_ref.quantize(e.reshape(128, 512).astype(BF)), q))
    return np.stack(o, axis=2).reshape(128, -1)
def f(rng, *shape):
    return mx_ref.flush((rng.standard_normal(shape, dtype=np.float32) * np.exp2(rng.integers(-2, 3, shape[:-1] + (1,)))).astype(BF))
def wide(rng, *shape, cols=0):
    v = rng.standard_normal(shape, dtype=np.float32) * np.exp2(rng.integers(-12, 13, shape)).astype(np.float32)
    if cols: v *= np.repeat(np.exp2(rng.integers(-cols, cols + 1, shape[:-2] + (1, shape[-1] // 4))) * (rng.random(shape[:-2] + (1, shape[-1] // 4)) > 0.0625), 4, axis=-1).astype(np.float32)
    return mx_ref.flush(v.astype(BF))
A, M, CAPP, R, O = 320, 32, 3, 3, 2
def flat(v):
    return np.concatenate([v[r] for r in range(N)], axis=1)
def ranks(v):
    return np.ascontiguousarray(v.reshape(128, N, -1).transpose(1, 0, 2))
def trim(v):
    v = np.asarray(v).astype(np.float32)
    v[np.abs(v) < np.float32(2.0 ** -16)] = 0
    return v.astype(BF)
def lists(rng):
    return np.stack([np.stack([rng.permutation(A)[:4] for i in range(M)], axis=1) for r in range(N)])
def given(rng, d, x, b, own):
    return {"d": d, "x": x, "b": b, "act": np.stack([table(v.reshape(-1)) for v in own]), "w": f(rng, N, 128, 512 * O)}
def setup_inputs(rng):
    d, own = trim(f(rng, N, 128, 4 * A)), lists(rng)
    every, x, b = flat(d), np.zeros((N, 128, 4 * M), np.float32), np.zeros((N, 128, 4 * M), np.float32)
    for r in range(N):
        for s in range(4): x[r] += np.float32(0.25) * cols(every, A * r + own[r, s]).astype(np.float32)
    x = trim(x)
    for r in range(N):
        b[r] = x[r].astype(np.float32)
        for k in range(3):
            g = rng.integers(0, N * A, M)
            if k == 0: g = np.where(rng.random(M) < 0.25, A * r + own[r, rng.integers(0, 4, M), np.arange(M)], g)
            b[r] += np.repeat(0.5 + rng.random(M), 4).astype(np.float32) * cols(every, g).astype(np.float32)
    return given(rng, d, x, trim(b), own)
def setup_inputs_crowd(rng):
    H, small = 6, np.float32(2.0 ** -10)
    rows = rng.permutation(512)[:H * N]
    hot = np.stack([A * q + rng.permutation(A)[:H] for q in range(N)])
    v = (flat(f(rng, N, 128, 4 * A)).astype(np.float32) * np.float32(0.125)).reshape(128, N * A, 4)
    v[rows // 4, :, rows % 4] = 0
    v[rows // 4, hot.reshape(-1), rows % 4] = 64
    x = f(rng, N, 128, 4 * M).astype(np.float32).reshape(N, 128, M, 4)
    x[:, rows // 4, :, rows % 4] = 0
    b, own, rows = x.copy(), np.zeros((N, 4, M), int), rows.reshape(N, H)
    busy = int(rng.integers(0, N))
    for r in range(N):
        flood = busy if r != busy else (busy + 1) % N
        even = int(rng.choice([q for q in range(N) if q != r and q != flood]))
        n = M // 8
        who = np.full(M, flood)
        who[:n] = -1
        who[n:n + CAPP + 2] = r
        who[n + CAPP + 2:n + 2 * CAPP + 2] = even
        who = rng.permutation(who)
        cold = np.setdiff1d(np.arange(A), hot[r] - A * r)
        for i in range(M):
            q, h = r if who[i] < 0 else int(who[i]), int(rng.integers(0, H))
            own[r, :, i] = rng.permutation(cold)[:4]
            if who[i] < 0: own[r, int(rng.integers(0, 4)), i] = hot[r, h] - A * r
            b[r, rows[q, h] // 4, i, rows[q, h] % 4] = 64
            k = rows[(q + int(rng.integers(1, N))) % N, int(rng.integers(0, H))]
            b[r, k // 4, i, k % 4] = 56
    return given(rng, ranks(trim(v * small)), trim((x * small).reshape(N, 128, 4 * M)), trim((b * small).reshape(N, 128, 4 * M)), own)
def setup_inputs_edge(rng):
    k = rng.integers(1, 8, (N * A, 4))
    v = np.zeros((128, N * A, 4))
    v[:64] = 2.0 ** 28
    for j in range(4):
        g = np.sort(rng.permutation(N * A)[:2])
        k[g[0], j], k[g[1], j] = 7, 8
        v[64 + 8 * j, :, 0] = k[:, j] * 2.0 ** 20
    v[96:] = rng.standard_normal((32, N * A, 4)) * 2.0 ** 20
    x = np.zeros((N, 128, M, 4))
    x[:, 96:] = rng.standard_normal((N, 32, M, 4)) * 2.0 ** 20
    b = x.copy()
    for r in range(N):
        u = np.where(rng.permutation(M) < M // 2, 2.0 ** 28, -(2.0 ** 28))
        x[r, :64] = -u[None, :, None]
        b[r, :64] = u[None, :, None]
        b[r, 64 + 8 * rng.integers(0, 4, M), np.arange(M), 0] = 2.0 ** 22
    return given(rng, ranks(trim(v)), trim(x.reshape(N, 128, 4 * M)), trim(b.reshape(N, 128, 4 * M)), lists(rng))
def setup_inputs_ties(rng):
    P = A // 8
    base = rng.standard_normal((128, P, 4))
    base[:, 0] = 0
    of = np.zeros((N, A), int)
    for q in range(N):
        first = np.arange(q, P, N)
        have = np.flatnonzero((np.arange(P) % N <= q) & (np.arange(P) > 0))
        of[q] = rng.permutation(np.concatenate([first, rng.choice(have, A - first.size)]))
    x = trim(rng.standard_normal((N, 128, M, 4)))
    b, own = x.astype(np.float32), lists(rng)
    for r in range(N):
        n = np.bincount(of[r], minlength=P)
        n[0] = 0
        p = int(np.argmax(n))
        spots = np.flatnonzero(of[r] == p)[1:]
        want, o = rng.integers(1, P, M), rng.permutation(M)
        for i in o[:M // 2]:
            want[i] = p
            own[r, :, i] = rng.permutation(spots)[:4]
        want[o[-1]] = 0
        if r == 0: own[0, :, int(o[-1])] = np.concatenate([[0], rng.permutation(np.flatnonzero(of[0] != of[0, 0]))[:3]])
        b[r] += (4 * base[:, want]).astype(np.float32)
    return given(rng, ranks(trim(base[:, of.reshape(-1)])), x.reshape(N, 128, 4 * M), trim(b.reshape(N, 128, 4 * M)), own)
def setup_inputs_spread(rng):
    return given(rng, trim(wide(rng, N, 128, 4 * A, cols=2)), trim(wide(rng, N, 128, 4 * M, cols=2)), trim(wide(rng, N, 128, 4 * M, cols=2)), lists(rng))
def check_inputs(d):
    bad = []
    for k, lo, hi in (("d", -16, 28), ("x", -16, 28), ("b", -16, 28), ("w", -30, 30)):
        v = np.abs(d[k].astype(np.float32))
        if not (np.isfinite(v).all() and ((v == 0) | (v >= 2.0 ** lo) & (v <= 2.0 ** hi)).all()): bad.append("a value of " + k)
    for r in range(N):
        a = entries(d["act"][r])
        if a.min() < 0 or a.max() >= A: bad.append("an entry of act")
        s = np.sort(a.reshape(4, M), axis=0)
        if (s[1:] == s[:-1]).any(): bad.append("two entries of act for one point are equal")
    return bad
def reference(d, x, b, act, w):
    every = mx_ref.quantize(np.ascontiguousarray(flat(d)))
    at, goal = flat(x).astype(np.float32), flat(b).astype(np.float32)
    own = np.stack([entries(act[r]).reshape(4, M).astype(np.int64) + A * r for r in range(N)])
    wq = [[mx_ref.quantize(np.ascontiguousarray(cut(w[r], o))) for o in range(O)] for r in range(N)]
    K = -(-N * M // 128)
    every_point = np.arange(M)
    y = np.zeros((N, 128, R * O * 4 * M), np.float32)
    for t in range(R):
        e = np.concatenate([(goal - at).astype(BF), np.zeros((128, 512 * K - 4 * N * M), BF)], axis=1)
        s = np.concatenate([mx_ref.matmul(mx_ref.quantize(np.ascontiguousarray(cut(e, k))), every) for k in range(K)])
        s = s[:N * M].reshape(N, M, N * A) + np.float32(0)
        far = np.argmax(s, axis=2)
        slot = np.stack([np.argmin(s[r, every_point, own[r]], axis=0) for r in range(N)])
        worst = np.stack([own[r, slot[r], every_point] for r in range(N)])
        go = np.zeros((N, M), bool)
        for r in range(N):
            used = np.zeros(N, int)
            for i in range(M):
                g = int(far[r, i])
                if (own[r, :, i] == g).any():
                    go[r, i] = True
                elif used[g // A] < CAPP:
                    used[g // A] += 1
                    go[r, i] = True
                    own[r, slot[r, i], i] = g
        v = decode(pick(every, np.concatenate([far.reshape(-1), worst.reshape(-1)]))).reshape(128, 2, N * M, 4)
        old = at.reshape(128, N * M, 4)
        new = ((v[:, 0] - v[:, 1]) * np.float32(0.25) + old).astype(BF).astype(np.float32)
        at = np.where(go.reshape(1, -1, 1), new, old).reshape(128, -1)
        for r in range(N):
            q = pick(every, own[r].reshape(-1))
            for o in range(O):
                i = (t * O + o) * 4 * M
                y[r, :, i:i + 4 * M] = mx_ref.matmul(wq[r][o], q)
    oc, osc = np.zeros((N, 128, 16 * M), np.uint8), np.zeros((N, 16, 4 * M), np.uint8)
    for r in range(N): oc[r], osc[r] = emit(pick(every, own[r].reshape(-1)))
    return {"y": y, "px": ranks(at), "oc": oc, "osc": osc, "an": own.astype(np.float32)}

@@ -1,0 +1,503 @@
+from concourse.bass import DstId, RemoteDMATransfer
+from concourse.mybir import dt, AluOpType, AxisListType, ActivationFunctionType
+
+N, A, M, CAPP, R, O = 8, 320, 32, 3, 3, 2
+G = N // 2
+NREL = 2
+PW = A // NREL
+BIG = 1.0e6
+CODE, F32, BF, I32, U8, U16 = "float8_e4m3fn_x4", "float32", "bfloat16", "int32", "uint8", "uint16"
+
+SCRATCH = {}
+for _n, _w in (("qd", A), ("at", G * A), ("rl", PW), ("es", 128 + 160 * R), ("fa", 64 * R + 128), ("ep", 512), ("en", 512),
+               ("wq", 128 * O), ("ca0", M), ("ca1", M), ("ca2", M), ("sl0", 192), ("sl1", 192), ("sl2", 192), ("sl3", 192)):
+    SCRATCH[_n + "c"] = ("sbuf", [128, _w], CODE)
+    SCRATCH[_n + "s"] = ("sbuf", [128, _w], U8)
+for _n, _w, _d in (("dtile", 4 * A, BF), ("xt", 128 * (R + 1), BF), ("bt", 128, BF), ("wt", 512 * O, BF), ("et", 512, BF), ("zt", 512, BF),
+                   ("ct", 2048, BF), ("zf", A, F32), ("rm", 2 * A, F32), ("sg", 2 * A, F32), ("ys", R * O * 128, F32), ("pxs", 128, F32),
+                   ("dl", 264, F32), ("io1", 128, I32), ("io2", 32, I32), ("io3", 32, I32), ("ia", 128, I32), ("ib", 128, I32),
+                   ("acti", 8, I32), ("m1", 32, F32), ("mt", 32, F32), ("mu", 32, F32), ("k16", 32, F32), ("k4", 32, F32),
+                   ("dg", 128, F32), ("pen", 40, F32), ("cs", 48, F32), ("kb", 72, F32), ("hw", 48, F32), ("kt", 32, F32), ("eq", 32, F32),
+                   ("xa", 96, F32), ("xb", 96, F32), ("xc", 96, F32), ("xd", 96, F32), ("sc", 384, F32),
+                   ("sm", 96, F32), ("h1", 12, F32), ("h2", 48, F32), ("anb", 32, F32), ("ant", 32, F32),
+                   ("mo", 8 * R, F32), ("mi", 2 * R, F32),
+                   ("oc2", 2, U16), ("oo", 2, U16), ("oa", 2, U16), ("of", 8, U16), ("ol", 8, U16)):
+    SCRATCH[_n] = ("sbuf", [128, _w], _d)
+SCRATCH["ps"] = ("psum", [128, 4096], F32)
+
+SEMAPHORES = (["vn", "sn", "tn", "gn", "sent", "ld0", "ld1", "lx", "lb", "la", "lw", "sty", "sts", "rc", "rs"]
+              + ["set%d" % k for k in range(G)]
+              + ["%s%d" % (s, t) for s in ("ee", "me", "cc", "cz") for t in range(R)])
+
+
+def bits(engines):
+    m = 0
+    for e in engines:
+        m |= 1 << e
+    return m
+
+
+def partners(T, topo):
+    free, out = list(range(G, N)), {}
+    for r in range(G):
+        q = [u for u in free if topo.may_write(T.cores[r], T.cores[u]) and topo.may_write(T.cores[u], T.cores[r])][0]
+        free.remove(q)
+        out[r], out[q] = q, r
+    return out
+
+
+def ways(T, topo, r):
+    c = T.cores[r]
+    group = [q for q in range(r // G * G, r // G * G + G) if q != r]
+    near = [q for q in group if topo.may_write(c, T.cores[q])]
+    far = [q for q in group if q not in near]
+    able = [u for u in topo.cores_of(c) if T.rank_of(u) is None and all(topo.may_write(u, T.cores[q]) for q in far)]
+    same = [u for u in able if topo.die(u) == topo.die(c)]
+    other = [u for u in able if u not in same]
+    relays = [u for two in zip(same, other) for u in two][:NREL]
+    return near, far, relays
+
+
+def send(g, T, topo, core, moves):
+    if len(moves) == 1:
+        d, o, i, s, e = moves[0]
+        rid, pid = topo.addr(d, core)
+        g.remote_dma(o, i, T.sem[s], T.sem.sent, pid, rid, bits(e))
+    else:
+        ts = []
+        for d, o, i, s, e in moves:
+            rid, pid = topo.addr(d, core)
+            ts.append(RemoteDMATransfer(dst_ids=[DstId(rid=rid, pnc=pid)], dma_engine_mask=bits(e), remote_sem=T.sem[s], src=i, dst=o))
+        g.remote_dma_fused(ts, local_sem=T.sem.sent)
+    return sum(len(m[4]) for m in moves)
+
+
+def share(engines, n, j):
+    w = len(engines) // n
+    return engines[j * w:j * w + w]
+
+
+def relay_program(g, core, T, topo, r, j):
+    near, far, relays = ways(T, topo, r)
+    got = len(share(topo.engines(T.cores[r], core), NREL, j))
+    lo = (r % G) * A + j * PW
+    n = 0
+    for sem, src, dst in (("rs", T.rls[:], T.ats[:, lo:lo + PW]), ("rc", T.rlc[:].bitcast(dt.uint8), T.atc[:, lo:lo + PW].bitcast(dt.uint8))):
+        g.wait_ge(T.sem[sem], got)
+        n += send(g, T, topo, core, [(T.cores[q], dst, src, "set%d" % (r % G), share(topo.engines(core, T.cores[q]), len(far), u))
+                                     for u, q in enumerate(far)])
+    g.wait_ge(T.sem.sent, n)
+
+
+def rank_program(g, core, T, topo):
+    rank = T.rank_of(core)
+    if rank is None:
+        for r in range(N):
+            relays = ways(T, topo, r)[2]
+            if core in relays:
+                relay_program(g, core, T, topo, r, relays.index(core))
+        return
+    k, grp = rank % G, rank // G
+    near, far, relays = ways(T, topo, rank)
+    mate = T.cores[partners(T, topo)[rank]]
+    em = topo.engines(core, mate)
+    Q = {"v": g.vector, "s": g.scalar, "t": g.tensor, "g": g, "y": g.sync}
+    seen = {q: {} for q in Q}
+    count = {"v": 0, "s": 0, "t": 0, "g": 0, "sent": 0, "sty": 0, "sts": 0}
+    log = {}
+    add, sub, mul, Op, Fn = AluOpType.add, AluOpType.subtract, AluOpType.mult, AluOpType, ActivationFunctionType
+
+    def rg(name, c0=0, c1=None, step=1, p0=0, p1=128):
+        return (name, p0, p1, c0, SCRATCH[name][1][1] if c1 is None else c1, step)
+
+    def q0(name, c0=0, c1=None, step=1):
+        return rg(name, c0, c1, step, 0, 32)
+
+    def h0(name, c0=0, c1=None, step=1):
+        return rg(name, c0, c1, step, 0, 64)
+
+    def ap(r):
+        if not isinstance(r, tuple):
+            return r
+        return T[r[0]][r[1]:r[2], r[3]:r[4]:r[5]] if r[5] != 1 else T[r[0]][r[1]:r[2], r[3]:r[4]]
+
+    def meet(a, b):
+        if a[0] == "ps":
+            return a[3] // 512 == b[3] // 512
+        if a[1] >= b[2] or b[1] >= a[2] or a[3] >= b[4] or b[3] >= a[4]:
+            return False
+        return not (a[5] == b[5] and (a[3] - b[3]) % a[5])
+
+    def wait(q, sem, n):
+        if seen[q].get(sem, 0) < n:
+            Q[q].wait_ge(T.sem[sem], n)
+            seen[q][sem] = n
+
+    def before(q, outs, ins):
+        need = {}
+        for r, w in [(r, True) for r in outs] + [(r, False) for r in ins if isinstance(r, tuple)]:
+            for r2, w2, q2, sem, n in log.get(r[0], ()):
+                if meet(r, r2) and ((q != q2) if r[0] == "ps" else (w or w2)):
+                    need[sem] = max(need.get(sem, 0), n)
+        for sem in sorted(need):
+            wait(q, sem, need[sem])
+
+    def note(q, outs, ins, sem, n):
+        for r, w in [(r, True) for r in outs] + [(r, False) for r in ins if isinstance(r, tuple)]:
+            log.setdefault(r[0], []).append((r, w, q, sem, n))
+
+    def run(q, outs, ins, call):
+        before(q, outs, ins)
+        count[q] += 1
+        call().then_inc(T.sem[q + "n"], 1)
+        note(q, outs, ins, q + "n", count[q])
+
+    def load(q, out, src, sem, n=16):
+        Q[q].dma_start(ap(out), src).then_inc(T.sem[sem], 16)
+        note(q, [out], [], sem, n)
+
+    def store(q, dst, src, view=None):
+        before(q, [], [src])
+        Q[q].dma_start(dst, view if view is not None else ap(src)).then_inc(T.sem["st" + q], 16)
+        count["st" + q] += 16
+
+    def post(srcs, moves):
+        before("g", [], srcs)
+        count["sent"] += send(g, T, topo, core, moves)
+
+    def u8(r):
+        return ap(r).bitcast(dt.uint8)
+
+    def ts(o, i, s1, op0, s2=None, op1=None):
+        if op1 is None:
+            run("v", [o], [i, s1], lambda: g.vector.tensor_scalar(ap(o), ap(i), ap(s1), None, op0))
+        else:
+            run("v", [o], [i, s1, s2], lambda: g.vector.tensor_scalar(ap(o), ap(i), ap(s1), ap(s2), op0, op1))
+
+    def tt(o, a, b, op):
+        run("v", [o], [a, b], lambda: g.vector.tensor_tensor(ap(o), ap(a), ap(b), op))
+
+    def red(o, i, op, neg=False):
+        run("v", [o], [i], lambda: g.vector.tensor_reduce(ap(o), ap(i), AxisListType.X, op, negate=neg))
+
+    def scan(o, a, b, first, op0, op1):
+        run("v", [o], [a, b], lambda: g.vector.tensor_tensor_scan(ap(o), ap(a), ap(b), first, op0, op1))
+
+    def cp(o, i):
+        run("v", [o], [i], lambda: g.vector.tensor_copy(ap(o), ap(i)))
+
+    def scp(o, i):
+        run("s", [o], [i], lambda: g.scalar.activation(ap(o), ap(i), Fn.Copy))
+
+    def ahead(o, i, last, n):
+        run("s", [o, n], [i], lambda: g.scalar.activation(ap(o), ap(i), Fn.Sign, bias=ap(last), scale=-1.0, accum_out=ap(n)))
+
+    def fill(o, v):
+        run("v", [o], [], lambda: g.vector.memset(ap(o), v))
+
+    def turn(o, i):
+        run("v", [o], [i], lambda: g.vector.transpose(ap(o), ap(i)))
+
+    def fold(x, keep, rows=q0):
+        turn(rows(x, 32, 64), rows(x, 0, 32))
+        return lambda: scan(rows(x, 64, 96), rows(keep), rows(x, 32, 64), 0.0, mul, add)
+
+    def quant(name, c0, c1, i):
+        c, s = rg(name + "c", c0, c1), rg(name + "s", c0, c1)
+        run("v", [c, s], [i], lambda: g.vector.quantize_mx(ap(c), ap(s), ap(i)))
+
+    def mm(bank, st, s0, mv, m0, n, start, stop):
+        o = rg("ps", 512 * bank, 512 * bank + n)
+        i = [rg(st + "c", s0, s0 + 128), rg(st + "s", s0, s0 + 128), rg(mv + "c", m0, m0 + n), rg(mv + "s", m0, m0 + n)]
+        run("t", [o], i, lambda: g.tensor.matmul_mx(ap(o), ap(i[0]), ap(i[1]), ap(i[2]), ap(i[3]), start, stop))
+
+    def pick(dst, d0, src, s0, s1, off):
+        n, f = 16 * SCRATCH[off][1][1], rg(off)
+        o, i = rg(dst + "c", d0, d0 + n), rg(src + "c", s0, s1)
+        run("v", [o], [i, f], lambda: g.vector.tensor_copy(ap(o).bitcast(dt.uint32), ap(i).bitcast(dt.uint32).indirect(ap(f))))
+        o2, i2 = rg(dst + "s", d0, d0 + n), rg(src + "s", s0, s1)
+        run("s", [o2], [i2, f], lambda: g.scalar.activation(ap(o2), ap(i2).indirect(ap(f)), Fn.Copy))
+
+    def spread(off, src, shift=None):
+        for a in range(4):
+            o = rg(off, p0=32 * a, p1=32 * a + 32)
+            if shift is None:
+                cp(o, src)
+            else:
+                ts(o, src, shift, add)
+
+    for q in range(grp * G, grp * G + G):
+        if q != rank:
+            qn, qf, qr = ways(T, topo, q)
+            if rank in qn:
+                n = 2 * len(topo.engines(T.cores[q], core))
+            else:
+                n = sum(2 * len(share(topo.engines(u, core), len(qf), 0)) for u in qr)
+            j = q % G
+            note("r", [rg("atc", j * A, j * A + A), rg("ats", j * A, j * A + A)], [], "set%d" % j, n)
+    ne = len(topo.engines(mate, core))
+    for t in range(R):
+        e0 = 128 + 160 * t
+        note("r", [rg("esc", e0, e0 + M), rg("ess", e0, e0 + M)], [], "ee%d" % t, 2 * ne)
+        note("r", [rg("mi", 2 * t, 2 * t + 2)], [], "me%d" % t, ne)
+        note("r", [rg("sl%dc" % t, M, 2 * M)], [], "cc%d" % t, ne)
+        note("r", [rg("sl%ds" % t, M, 2 * M)], [], "cz%d" % t, ne)
+
+    H = 2 * A
+    load("y", rg("dtile", 0, H), T.d[:, 0:H], "ld0")
+    load("s", rg("dtile", H, 2 * H), T.d[:, H:2 * H], "ld1")
+    load("y", rg("xt", 0, 128), T.x[:, :], "lx")
+    load("s", rg("bt"), T.b[:, :], "lb")
+    load("y", rg("acti", p0=0, p1=16), T.act[:, :], "la", 32)
+    load("y", rg("acti", p0=16, p1=32), T.act[:, :], "la", 32)
+    run("g", [rg("io1")], [], lambda: g.iota(T.io1[:], [[-1, 128]], 128, 1))
+    run("g", [rg("io2")], [], lambda: g.iota(T.io2[:], [[1, 32]], 0, 0))
+    run("g", [rg("io3")], [], lambda: g.iota(T.io3[:], [[0, 2], [1, 4], [0, 4]], 128, -1))
+    for name in ("et", "zt", "mo", "anb", "zf"):
+        fill(rg(name), 0.0)
+    fill(rg("dl", 256, 264), 0.0)
+
+    quant("qd", 0, A // 2, rg("dtile", 0, H))
+    quant("qd", A // 2, A, rg("dtile", H, 2 * H))
+    for x, view, sem in (("s", ap, "rs"), ("c", u8, "rc")):
+        post([rg("qd" + x)], [(u, view(rg("rl" + x)), view(rg("qd" + x, j * PW, j * PW + PW)), sem, share(topo.engines(core, u), NREL, j))
+                              for j, u in enumerate(relays)])
+    for x, view in (("c", u8), ("s", ap)):
+        for q in near:
+            post([rg("qd" + x)], [(T.cores[q], view(rg("at" + x, k * A, k * A + A)), view(rg("qd" + x)), "set%d" % k, topo.engines(core, T.cores[q]))])
+
+    def send_e(t):
+        e0 = 128 + 160 * t
+        tt(rg("et", 0, 128), rg("bt"), rg("xt", 128 * t, 128 * t + 128), sub)
+        quant("es", e0 + M, e0 + 160, rg("et"))
+        for x, view in (("c", u8), ("s", ap)):
+            src = rg("es" + x, e0 + M, e0 + 2 * M)
+            post([src], [(mate, view(rg("es" + x, e0, e0 + M)), view(src), "ee%d" % t, em)])
+
+    send_e(0)
+    quant("at", k * A, k * A + A, rg("dtile"))
+    quant("es", 0, 128, rg("zt"))
+    quant("fa", 64 * R, 64 * R + 128, rg("zt"))
+    fill(rg("ct"), 0.0)
+
+    def cs(c, n=1, rows=q0):
+        return rows("cs", c, c + n)
+
+    def sm(c, n=1, rows=q0):
+        return rows("sm", c, c + n)
+
+    U, THR, NEG4, STEP5, BASEP, HI, PM, P4, PI, PF = cs(0), cs(1, 7), cs(8, 4), cs(32, 5, h0), cs(16, 8), cs(24), cs(25), cs(26), cs(27), cs(28)
+    P128 = q0("io1", 0, 1)
+    ts(h0("ia", 0, 32), h0("io1", 0, 32), 15, Op.bitwise_and)
+    ts(q0("ib"), q0("io1"), 31, Op.bitwise_and)
+    ts(q0("ia", 32, 64), q0("io3"), 3, Op.bitwise_and)
+    ts(h0("ia", 64, 96), h0("io2"), 15, Op.bitwise_and)
+    ts(q0("ia", 96, 128), q0("io2"), 3, Op.bitwise_and)
+    ts(q0("pen", 0, 33), q0("io1", 0, 33), 128.0, Op.is_gt, 1000.0, mul)
+    ts(U, P128, 8.0, mul, 16.0 - 8 * 128, add)
+    ts(HI, P128, 128.0 + 16, Op.is_ge)
+    ts(PI, P128, -128.0 - 64, add)
+    ts(PF, P128, 4.0, mul, -4.0 * (128 + 64), add)
+    ts(THR, q0("io2", 0, 7), float(A), mul, float(A), add)
+    ts(h0("m1"), h0("ia", 0, 32), 0.0, Op.is_equal)
+    ts(q0("dg"), q0("ib"), 0.0, Op.is_gt, 1.0e29, mul)
+    ts(q0("mu"), q0("ia", 32, 64), 0.0, Op.is_equal, CAPP + 1.5, mul)
+    ts(h0("k16"), h0("ia", 64, 96), 0.0, Op.is_gt)
+    ts(q0("k4"), q0("ia", 96, 128), 0.0, Op.is_gt)
+    cp(PM, q0("ia", 0, 1))
+    ts(q0("ia", 33, 34), q0("ia", 0, 1), 3, Op.bitwise_and)
+    ts(q0("mt"), q0("m1"), CAPP + 1.5, mul, -1.0, add)
+    ts(q0("mu"), q0("mu"), -1.0, add)
+    ts(BASEP, q0("io2", 0, 8), 16.0, mul, PM, add)
+    ts(NEG4, q0("io2", 0, 4), -32.0, mul, PI, sub)
+    ts(P4, q0("ia", 33, 34), 256.0, add)
+    ts(NEG4, NEG4, -64.0, add)
+    fill(q0("hw"), 1.0)
+    cp(q0("h2", 13, 14), q0("pen", 0, 1))
+    tt(q0("h2", 14, 46), q0("pen", 1, 33), q0("pen", 0, 32), sub)
+    fill(cs(32, 4, h0), float(A))
+    fill(cs(36, 1, h0), float(G * A * grp))
+    fill(sm(44, 1, h0), 4 * BIG)
+    for name, v in (("en", -0.25), ("ep", 0.25)):
+        for b in range(4):
+            ts(rg("ct", 512 * b + b, 512 * b + 512, 4), rg("io1"), 128.0, Op.is_equal, v, mul)
+        quant(name, 0, 512, rg("ct"))
+
+    AN = q0("anb", 0, 4)
+    spread("ol", q0("acti"))
+    pick("sl0", 64, "at", k * A, k * A + A, "ol")
+    tt(sm(0, 4), q0("acti", 1, 8, 2), q0("acti", 0, 8, 2), sub)
+    ts(sm(4, 4), sm(0, 4), HI, mul, float(A * rank), add)
+    tt(AN, sm(4, 4), q0("acti", 0, 8, 2), add)
+
+    NPOS, HOT, C0 = sm(20), sm(21, 4), sm(25)
+    V4, PEN4, KEY5 = sm(28, 4, h0), sm(36, 4, h0), sm(40, 5, h0)
+    OWNN, OWNV, DCOL, CNT, DM, WC = sm(46), sm(47), sm(52), sm(53), sm(54), sm(55)
+    DN, MISS, FET, OF4, T4, T5, L8, L9 = sm(60), sm(61), sm(62), sm(64, 4), sm(68, 4), sm(72, 4), sm(76, 8), sm(84, 8)
+    KEY, NKEY, KEY1, WIN = q0("kb", 64, 65), q0("h2", 11, 12), q0("h2", 12, 13), q0("hw", 12, 13)
+
+    def worst(t):
+        mm(6, "es", 128 + 160 * t + M, "sl%d" % t, 64, 128, True, True)
+        tt(q0("sc", 0, 128), q0("ps", 3072, 3200), q0("dg"), add)
+        scan(q0("sc", 128, 256), q0("sc", 0, 128), q0("sc", 0, 128), 5.0e29, Op.min, Op.min)
+        ahead(q0("sc", 256, 384), q0("sc", 128, 256), q0("sc", 255, 256), NPOS)
+        ts(q0("xa", 0, 32), q0("m1"), NPOS, mul, -1.0, mul)
+        ts(HOT, NEG4, NPOS, Op.is_equal)
+        later = fold("xa", "k16")
+        tt(C0, NPOS, PI, add)
+        later()
+
+    def products(t):
+        for o in range(O):
+            mm(o, "wq", 128 * o, "sl%d" % (t + 1), 64, 128, True, True)
+        for o in range(O):
+            scp(rg("ys", (t * O + o) * 128, (t * O + o + 1) * 128), rg("ps", 512 * o, 512 * o + 128))
+
+    def score(t):
+        e0 = 128 + 160 * t
+        order = (k % 2, 1 - k % 2)
+        for c in order:
+            mm(c, "es", e0, "at", c * A, A, True, False)
+            mm(c, "es", e0 - 64, "at", (2 + c) * A, A, False, True)
+        for c in order:
+            u = 1 - c
+            o = rg("rm", u * A, u * A + A)
+            scan(o, rg("ps", 512 * c, 512 * c + A), rg("zf"), -1.0e29, Op.max, add)
+            ahead(rg("sg", u * A, u * A + A), o, rg("rm", u * A + A - 1, u * A + A), rg("sm", 26 + u, 27 + u))
+        if t:
+            products(t - 1)
+        num, top = h0("mo", 8 * t + 4, 8 * t + 5), h0("mo", 8 * t + 5, 8 * t + 6)
+        cp(sm(30, 2, h0), h0("rm", A - 1, 2 * A, A))
+        cp(sm(28, 2, h0), rg("rm", A - 1, 2 * A, A, 64, 128))
+        red(top, V4, Op.max)
+        ts(PEN4, V4, top, Op.is_lt, BIG, mul)
+        tt(sm(42, 2, h0), sm(26, 2, h0), sm(38, 2, h0), add)
+        tt(sm(40, 2, h0), rg("sm", 26, 28, 1, 64, 128), sm(36, 2, h0), add)
+        scan(h0("mo", 8 * t, 8 * t + 5), STEP5, KEY5, BIG, add, Op.min)
+        src = rg("mo", 8 * t + 4, 8 * t + 6)
+        post([src], [(mate, ap(rg("mi", 2 * t, 2 * t + 2)), ap(src), "me%d" % t, em)])
+        ts(h0("xc", 0, 32), h0("m1"), num, mul)
+        cp(sm(46, 2), rg("mo", 8 * t + 4, 8 * t + 6, 1, 32, 64))
+        later = fold("xc", "k16", h0)
+        ts(q0("h1", 0, 4), AN, OWNN, Op.is_equal, U, mul)
+        later()
+        ts(q0("h1", 4, 11), THR, OWNN, Op.is_le)
+        spread("oc2", q0("xc", 79, 96, 16), float(-G * A * grp))
+        red(NKEY, q0("h1", 0, 11), add, True)
+        pick("ca%d" % t, 0, "at", 0, G * A, "oc2")
+        for x, view, sem in (("c", u8, "cc"), ("s", ap, "cz")):
+            src = rg("ca%d%s" % (t, x))
+            post([src], [(mate, view(rg("sl%d%s" % (t, x), M, 2 * M)), view(src), "%s%d" % (sem, t), em)])
+
+    def prepare(t):
+        f0 = 64 * (R - 1 - t)
+        red(KEY1, q0("h1", 0, 11), add)
+        spread("oa", q0("xa", 79, 96, 16))
+        spread("oo", rg("xc", 79, 96, 16, 32, 64), float(-G * A * grp))
+        pick("fa", f0, "sl%d" % t, 64, 192, "oa")
+        pick("fa", f0 + M, "sl%d" % t, 64, 192, "oa")
+        pick("sl%d" % t, 0, "at", 0, G * A, "oo")
+        for b in range(4):
+            mm(2 + b, "en", 128 * b, "fa", f0, 128, True, False)
+        for b in range(4):
+            mm(2 + b, "ep", 128 * b, "sl%d" % t, 0, 128, False, True)
+        for b in range(4):
+            scp(rg("dl", b, 256, 4), rg("ps", 1024 + 512 * b, 1024 + 512 * b + 64))
+
+    def decide(t):
+        n2, v2 = q0("mi", 2 * t, 2 * t + 1), q0("mi", 2 * t + 1, 2 * t + 2)
+        ts(q0("h2", 0, 4), AN, n2, Op.is_equal, U, mul)
+        ts(q0("h2", 4, 11), THR, n2, Op.is_le)
+        ts(WIN, v2, OWNV, Op.is_ge if grp else Op.is_gt)
+        scan(q0("kb", 19, 65), q0("hw", 0, 46), q0("h2", 0, 46), 0.0, mul, add)
+        ts(DCOL, WIN, 32.0, mul, C0, add)
+        turn(q0("kt"), q0("kb", 32, 64))
+        ts(WC, WIN, 128.0, mul, PF, add)
+        ts(q0("eq"), q0("kt"), KEY, Op.is_equal)
+        ts(MISS, KEY, float(N), Op.is_lt)
+        red(CNT, q0("eq"), add)
+        ts(DM, KEY, float(N), Op.is_lt, DCOL, mul)
+
+    def step(t):
+        o, i, w, f = rg("xt", 128 * t + 128, 128 * t + 256), rg("xt", 128 * t, 128 * t + 128), rg("dl"), rg("of")
+        run("v", [o], [i, w, f], lambda: g.vector.tensor_tensor(ap(o), ap(w).indirect(ap(f)), ap(i), add))
+
+    def changed():
+        for c in range(2):
+            ts(q0("sm", 76 + c, 84, 2), q0("cs", 16 + c, 24, 2), q0("xa", 79 + 16 * c, 80 + 16 * c), Op.is_equal, q0("xd", 79 + 16 * c, 80 + 16 * c), mul)
+
+    def move(t):
+        ts(q0("xb", 0, 32), q0("mu"), CNT, Op.is_gt, WC, mul)
+        ts(FET, CNT, CAPP + 0.5, Op.is_lt, MISS, mul)
+        later = fold("xb", "k4")
+        ts(OF4, HOT, FET, mul)
+        later()
+        ts(DN, q0("mi", 2 * t, 2 * t + 1), OWNN, sub, WIN, mul)
+        spread("of", q0("xb", 67, 96, 4), P4)
+        ts(T4, AN, OWNN, sub, DN, sub)
+        step(t)
+
+    def slots(t):
+        ts(q0("xd", 0, 32), q0("mt"), CNT, Op.is_gt, DM, mul)
+        tt(T5, T4, OF4, mul)
+        later = fold("xd", "k16")
+        tt(AN, AN, T5, sub)
+        later()
+        changed()
+        tt(L9, L8, BASEP, add)
+        spread("ol", L9, 64.0)
+        pick("sl%d" % (t + 1), 64, "sl%d" % t, 0, 192, "ol")
+
+    def finish(t):
+        last = "sl%d" % R
+        ts(q0("xd", 0, 32), q0("mt"), CNT, Op.is_gt, DM, mul)
+        ts(q0("xb", 0, 32), q0("mu"), CNT, Op.is_gt, WC, mul)
+        sums = [fold("xd", "k16"), fold("xb", "k4")]
+        sums[0]()
+        sums[1]()
+        changed()
+        ts(DN, q0("mi", 2 * t, 2 * t + 1), OWNN, sub, WIN, mul)
+        ts(FET, CNT, CAPP + 0.5, Op.is_lt, MISS, mul)
+        tt(L9, L8, BASEP, add)
+        ts(OF4, HOT, FET, mul)
+        spread("ol", L9, 64.0)
+        ts(T4, AN, OWNN, sub, DN, sub)
+        pick(last, 64, "sl%d" % t, 0, 192, "ol")
+        store("y", T.oc[:, :], rg(last + "c", 64, 192), u8(rg(last + "c", 64, 192)))
+        spread("of", q0("xb", 67, 96, 4), P4)
+        tt(T5, T4, OF4, mul)
+        products(t)
+        store("s", T.y[:, 256 * t:256 * t + 256], rg("ys", 256 * t, 256 * t + 256))
+        step(t)
+        tt(AN, AN, T5, sub)
+        cp(rg("pxs"), rg("xt", 128 * R, 128 * R + 128))
+        turn(q0("ant"), q0("anb"))
+        for a in range(4):
+            store("y", T.osc[4 * a:4 * a + 4, :], rg(last + "s", 64, 192, 1, 32 * a, 32 * a + 4))
+        store("y", T.px[:, :], rg("pxs"))
+        store("s", T.an[:, :], rg("ant", 0, 32, 1, 0, 4))
+
+    for t in range(R):
+        worst(t)
+        if t == 0:
+            wait("y", "set%d" % (near[0] % G), 2 * len(topo.engines(T.cores[near[0]], core)))
+            load("y", rg("wt"), T.w[:, :], "lw")
+        score(t)
+        prepare(t)
+        if t:
+            wait("y", "cz%d" % t, ne)
+            store("y", T.y[:, 256 * (t - 1):256 * t], rg("ys", 256 * (t - 1), 256 * t))
+        else:
+            quant("wq", 0, 128 * O, rg("wt"))
+        decide(t)
+        if t < R - 1:
+            move(t)
+            send_e(t + 1)
+            slots(t)
+        else:
+            finish(t)
+    for q in "vstg":
+        wait("g", q + "n", count[q])
+    wait("g", "sent", count["sent"])
+    wait("y", "sty", count["sty"])
+    wait("s", "sts", count["sts"])

@@ -2,9 +2,10 @@ from concourse.bass import DstId, RemoteDMATransfer
 from concourse.mybir import dt, AluOpType, AxisListType, ActivationFunctionType
 
 N, A, M, CAPP, R, O = 8, 320, 32, 3, 3, 2
+CORES = 256
 G = N // 2
-NREL = 2
-PW = A // NREL
+NREL = 4
+PW = A // 2
 BIG = 1.0e6
 CODE, F32, BF, I32, U8, U16 = "float8_e4m3fn_x4", "float32", "bfloat16", "int32", "uint8", "uint16"
 
@@ -15,7 +16,7 @@ for _n, _w in (("qd", A), ("at", G * A), ("rl", PW), ("es", 128 + 160 * R), ("fa
     SCRATCH[_n + "s"] = ("sbuf", [128, _w], U8)
 for _n, _w, _d in (("dtile", 4 * A, BF), ("xt", 128 * (R + 1), BF), ("bt", 128, BF), ("wt", 512 * O, BF), ("et", 512, BF), ("zt", 512, BF),
                    ("ct", 2048, BF), ("zf", A, F32), ("rm", 2 * A, F32), ("sg", 2 * A, F32), ("ys", R * O * 128, F32), ("pxs", 128, F32),
-                   ("dl", 264, F32), ("io1", 128, I32), ("io2", 32, I32), ("io3", 32, I32), ("ia", 128, I32), ("ib", 128, I32),
+                   ("idt", 128, BF), ("dl", 264, F32), ("io1", 128, I32), ("io2", 32, I32), ("io3", 32, I32), ("ia", 128, I32), ("ib", 128, I32),
                    ("acti", 8, I32), ("m1", 32, F32), ("mt", 32, F32), ("mu", 32, F32), ("k16", 32, F32), ("k4", 32, F32),
                    ("dg", 128, F32), ("pen", 40, F32), ("cs", 48, F32), ("kb", 72, F32), ("hw", 48, F32), ("kt", 32, F32), ("eq", 32, F32),
                    ("xa", 96, F32), ("xb", 96, F32), ("xc", 96, F32), ("xd", 96, F32), ("sc", 384, F32),
@@ -51,11 +52,27 @@ def ways(T, topo, r):
     group = [q for q in range(r // G * G, r // G * G + G) if q != r]
     near = [q for q in group if topo.may_write(c, T.cores[q])]
     far = [q for q in group if q not in near]
-    able = [u for u in topo.cores_of(c) if T.rank_of(u) is None and all(topo.may_write(u, T.cores[q]) for q in far)]
-    same = [u for u in able if topo.die(u) == topo.die(c)]
-    other = [u for u in able if u not in same]
-    relays = [u for two in zip(same, other) for u in two][:NREL]
-    return near, far, relays
+    home = [u for u in topo.cores_of(c) if topo.die(u) != topo.die(c) and all(topo.may_write(u, T.cores[q]) for q in far)]
+    away = []
+    for q in far:
+        d = T.cores[q]
+        able = [u for u in range(CORES) if topo.mates(u, d) and topo.may_write(u, d) and topo.may_write(c, u)]
+        same = [u for u in able if topo.die(u) == topo.die(c)]
+        other = [u for u in able if u not in same]
+        away.append((same, other)[sorted([r] + near).index(r)][0])
+    return near, far, away + home[:2]
+
+
+def share(engines, n, j):
+    w = len(engines) // n
+    return engines[j * w:j * w + w]
+
+
+def job(T, topo, r, j):
+    near, far, relays = ways(T, topo, r)
+    off = topo.engines(T.cores[r], relays[0])
+    use = off if j < 2 else [e for e in topo.engines(T.cores[r], relays[j]) if e not in off]
+    return j // 2, far[j % 2], share(use, 2, j % 2)
 
 
 def send(g, T, topo, core, moves):
@@ -72,20 +89,13 @@ def send(g, T, topo, core, moves):
     return sum(len(m[4]) for m in moves)
 
 
-def share(engines, n, j):
-    w = len(engines) // n
-    return engines[j * w:j * w + w]
-
-
 def relay_program(g, core, T, topo, r, j):
-    near, far, relays = ways(T, topo, r)
-    got = len(share(topo.engines(T.cores[r], core), NREL, j))
-    lo = (r % G) * A + j * PW
+    half, to, got = job(T, topo, r, j)
+    lo = (r % G) * A + half * PW
     n = 0
     for sem, src, dst in (("rs", T.rls[:], T.ats[:, lo:lo + PW]), ("rc", T.rlc[:].bitcast(dt.uint8), T.atc[:, lo:lo + PW].bitcast(dt.uint8))):
-        g.wait_ge(T.sem[sem], got)
-        n += send(g, T, topo, core, [(T.cores[q], dst, src, "set%d" % (r % G), share(topo.engines(core, T.cores[q]), len(far), u))
-                                     for u, q in enumerate(far)])
+        g.wait_ge(T.sem[sem], len(got))
+        n += send(g, T, topo, core, [(T.cores[to], dst, src, "set%d" % (r % G), topo.engines(core, T.cores[to]))])
     g.wait_ge(T.sem.sent, n)
 
 
@@ -189,6 +199,9 @@ def rank_program(g, core, T, topo):
     def scp(o, i):
         run("s", [o], [i], lambda: g.scalar.activation(ap(o), ap(i), Fn.Copy))
 
+    def fma(o, i, scale, bias):
+        run("s", [o], [i, scale, bias], lambda: g.scalar.activation(ap(o), ap(i), Fn.Identity, bias=ap(bias), scale=ap(scale)))
+
     def ahead(o, i, last, n):
         run("s", [o, n], [i], lambda: g.scalar.activation(ap(o), ap(i), Fn.Sign, bias=ap(last), scale=-1.0, accum_out=ap(n)))
 
@@ -232,7 +245,7 @@ def rank_program(g, core, T, topo):
             if rank in qn:
                 n = 2 * len(topo.engines(T.cores[q], core))
             else:
-                n = sum(2 * len(share(topo.engines(u, core), len(qf), 0)) for u in qr)
+                n = sum(2 * len(topo.engines(u, core)) for i, u in enumerate(qr) if job(T, topo, q, i)[1] == rank)
             j = q % G
             note("r", [rg("atc", j * A, j * A + A), rg("ats", j * A, j * A + A)], [], "set%d" % j, n)
     ne = len(topo.engines(mate, core))
@@ -245,40 +258,24 @@ def rank_program(g, core, T, topo):
 
     H = 2 * A
     load("y", rg("dtile", 0, H), T.d[:, 0:H], "ld0")
-    load("s", rg("dtile", H, 2 * H), T.d[:, H:2 * H], "ld1")
+    load("y", rg("dtile", H, 2 * H), T.d[:, H:2 * H], "ld1")
     load("y", rg("xt", 0, 128), T.x[:, :], "lx")
-    load("s", rg("bt"), T.b[:, :], "lb")
-    load("y", rg("acti", p0=0, p1=16), T.act[:, :], "la", 32)
-    load("y", rg("acti", p0=16, p1=32), T.act[:, :], "la", 32)
+    load("y", rg("bt"), T.b[:, :], "lb")
+    load("s", rg("acti", p0=0, p1=16), T.act[:, :], "la", 32)
+    load("s", rg("acti", p0=16, p1=32), T.act[:, :], "la", 32)
     run("g", [rg("io1")], [], lambda: g.iota(T.io1[:], [[-1, 128]], 128, 1))
     run("g", [rg("io2")], [], lambda: g.iota(T.io2[:], [[1, 32]], 0, 0))
     run("g", [rg("io3")], [], lambda: g.iota(T.io3[:], [[0, 2], [1, 4], [0, 4]], 128, -1))
-    for name in ("et", "zt", "mo", "anb", "zf"):
+    fill(rg("zt"), 0.0)
+    for name, n in (("et", 512), ("zf", A)):
+        scp(rg(name), rg("zt", 0, n))
+    for b in range(4):
+        scp(rg("ct", 512 * b, 512 * b + 512), rg("zt"))
+    for name in ("mo", "anb"):
         fill(rg(name), 0.0)
     fill(rg("dl", 256, 264), 0.0)
-
-    quant("qd", 0, A // 2, rg("dtile", 0, H))
-    quant("qd", A // 2, A, rg("dtile", H, 2 * H))
-    for x, view, sem in (("s", ap, "rs"), ("c", u8, "rc")):
-        post([rg("qd" + x)], [(u, view(rg("rl" + x)), view(rg("qd" + x, j * PW, j * PW + PW)), sem, share(topo.engines(core, u), NREL, j))
-                              for j, u in enumerate(relays)])
-    for x, view in (("c", u8), ("s", ap)):
-        for q in near:
-            post([rg("qd" + x)], [(T.cores[q], view(rg("at" + x, k * A, k * A + A)), view(rg("qd" + x)), "set%d" % k, topo.engines(core, T.cores[q]))])
-
-    def send_e(t):
-        e0 = 128 + 160 * t
-        tt(rg("et", 0, 128), rg("bt"), rg("xt", 128 * t, 128 * t + 128), sub)
-        quant("es", e0 + M, e0 + 160, rg("et"))
-        for x, view in (("c", u8), ("s", ap)):
-            src = rg("es" + x, e0 + M, e0 + 2 * M)
-            post([src], [(mate, view(rg("es" + x, e0, e0 + M)), view(src), "ee%d" % t, em)])
-
-    send_e(0)
-    quant("at", k * A, k * A + A, rg("dtile"))
     quant("es", 0, 128, rg("zt"))
     quant("fa", 64 * R, 64 * R + 128, rg("zt"))
-    fill(rg("ct"), 0.0)
 
     def cs(c, n=1, rows=q0):
         return rows("cs", c, c + n)
@@ -300,12 +297,40 @@ def rank_program(g, core, T, topo):
     ts(PF, P128, 4.0, mul, -4.0 * (128 + 64), add)
     ts(THR, q0("io2", 0, 7), float(A), mul, float(A), add)
     ts(h0("m1"), h0("ia", 0, 32), 0.0, Op.is_equal)
-    ts(q0("dg"), q0("ib"), 0.0, Op.is_gt, 1.0e29, mul)
-    ts(q0("mu"), q0("ia", 32, 64), 0.0, Op.is_equal, CAPP + 1.5, mul)
-    ts(h0("k16"), h0("ia", 64, 96), 0.0, Op.is_gt)
-    ts(q0("k4"), q0("ia", 96, 128), 0.0, Op.is_gt)
-    cp(PM, q0("ia", 0, 1))
-    ts(q0("ia", 33, 34), q0("ia", 0, 1), 3, Op.bitwise_and)
+
+    jobs = [job(T, topo, rank, j) for j in range(NREL)]
+    for h in range(2):
+        quant("qd", h * PW, h * PW + PW, rg("dtile", h * H, h * H + H))
+        for x, view, sem in (("s", ap, "rs"), ("c", u8, "rc")):
+            src = rg("qd" + x, h * PW, h * PW + PW)
+            post([src], [(relays[j], view(rg("rl" + x)), view(src), sem, jobs[j][2]) for j in range(NREL) if jobs[j][0] == h])
+        if h == 0:
+            ts(q0("dg"), q0("ib"), 0.0, Op.is_gt, 1.0e29, mul)
+            ts(q0("mu"), q0("ia", 32, 64), 0.0, Op.is_equal, CAPP + 1.5, mul)
+            ts(h0("k16"), h0("ia", 64, 96), 0.0, Op.is_gt)
+            ts(q0("k4"), q0("ia", 96, 128), 0.0, Op.is_gt)
+            cp(PM, q0("ia", 0, 1))
+            ts(q0("ia", 33, 34), q0("ia", 0, 1), 3, Op.bitwise_and)
+    for x, view in (("c", u8), ("s", ap)):
+        for q in near:
+            post([rg("qd" + x)], [(T.cores[q], view(rg("at" + x, k * A, k * A + A)), view(rg("qd" + x)), "set%d" % k, topo.engines(core, T.cores[q]))])
+
+    def send_e(t):
+        e0 = 128 + 160 * t
+        tt(rg("et", 0, 128), rg("bt"), rg("xt", 128 * t, 128 * t + 128), sub)
+        quant("es", e0 + M, e0 + 160, rg("et"))
+        for x, view in (("c", u8), ("s", ap)):
+            src = rg("es" + x, e0 + M, e0 + 2 * M)
+            post([src], [(mate, view(rg("es" + x, e0, e0 + M)), view(src), "ee%d" % t, em)])
+
+    def tile(v):
+        for b in range(4):
+            fma(rg("ct", 512 * b + b, 512 * b + 512, 4), rg("idt"), v, 0.0)
+
+    quant("at", k * A, k * A + A, rg("dtile"))
+    ts(rg("idt"), rg("io1"), 128.0, Op.is_equal)
+    send_e(0)
+    tile(-0.25)
     ts(q0("mt"), q0("m1"), CAPP + 1.5, mul, -1.0, add)
     ts(q0("mu"), q0("mu"), -1.0, add)
     ts(BASEP, q0("io2", 0, 8), 16.0, mul, PM, add)
@@ -318,10 +343,6 @@ def rank_program(g, core, T, topo):
     fill(cs(32, 4, h0), float(A))
     fill(cs(36, 1, h0), float(G * A * grp))
     fill(sm(44, 1, h0), 4 * BIG)
-    for name, v in (("en", -0.25), ("ep", 0.25)):
-        for b in range(4):
-            ts(rg("ct", 512 * b + b, 512 * b + 512, 4), rg("io1"), 128.0, Op.is_equal, v, mul)
-        quant(name, 0, 512, rg("ct"))
 
     AN = q0("anb", 0, 4)
     spread("ol", q0("acti"))
@@ -329,6 +350,8 @@ def rank_program(g, core, T, topo):
     tt(sm(0, 4), q0("acti", 1, 8, 2), q0("acti", 0, 8, 2), sub)
     ts(sm(4, 4), sm(0, 4), HI, mul, float(A * rank), add)
     tt(AN, sm(4, 4), q0("acti", 0, 8, 2), add)
+    quant("en", 0, 512, rg("ct"))
+    tile(0.25)
 
     NPOS, HOT, C0 = sm(20), sm(21, 4), sm(25)
     V4, PEN4, KEY5 = sm(28, 4, h0), sm(36, 4, h0), sm(40, 5, h0)
@@ -341,11 +364,7 @@ def rank_program(g, core, T, topo):
         tt(q0("sc", 0, 128), q0("ps", 3072, 3200), q0("dg"), add)
         scan(q0("sc", 128, 256), q0("sc", 0, 128), q0("sc", 0, 128), 5.0e29, Op.min, Op.min)
         ahead(q0("sc", 256, 384), q0("sc", 128, 256), q0("sc", 255, 256), NPOS)
-        ts(q0("xa", 0, 32), q0("m1"), NPOS, mul, -1.0, mul)
-        ts(HOT, NEG4, NPOS, Op.is_equal)
-        later = fold("xa", "k16")
-        tt(C0, NPOS, PI, add)
-        later()
+        fma(C0, NPOS, 1.0, PI)
 
     def products(t):
         for o in range(O):
@@ -369,10 +388,14 @@ def rank_program(g, core, T, topo):
         num, top = h0("mo", 8 * t + 4, 8 * t + 5), h0("mo", 8 * t + 5, 8 * t + 6)
         cp(sm(30, 2, h0), h0("rm", A - 1, 2 * A, A))
         cp(sm(28, 2, h0), rg("rm", A - 1, 2 * A, A, 64, 128))
+        ts(q0("xa", 0, 32), q0("m1"), NPOS, mul, -1.0, mul)
         red(top, V4, Op.max)
+        after = fold("xa", "k16")
         ts(PEN4, V4, top, Op.is_lt, BIG, mul)
+        after()
         tt(sm(42, 2, h0), sm(26, 2, h0), sm(38, 2, h0), add)
         tt(sm(40, 2, h0), rg("sm", 26, 28, 1, 64, 128), sm(36, 2, h0), add)
+        ts(HOT, NEG4, NPOS, Op.is_equal)
         scan(h0("mo", 8 * t, 8 * t + 5), STEP5, KEY5, BIG, add, Op.min)
         src = rg("mo", 8 * t + 4, 8 * t + 6)
         post([src], [(mate, ap(rg("mi", 2 * t, 2 * t + 2)), ap(src), "me%d" % t, em)])
@@ -391,7 +414,7 @@ def rank_program(g, core, T, topo):
 
     def prepare(t):
         f0 = 64 * (R - 1 - t)
-        red(KEY1, q0("h1", 0, 11), add)
+        fma(KEY1, NKEY, -1.0, 0.0)
         spread("oa", q0("xa", 79, 96, 16))
         spread("oo", rg("xc", 79, 96, 16, 32, 64), float(-G * A * grp))
         pick("fa", f0, "sl%d" % t, 64, 192, "oa")
@@ -401,8 +424,6 @@ def rank_program(g, core, T, topo):
             mm(2 + b, "en", 128 * b, "fa", f0, 128, True, False)
         for b in range(4):
             mm(2 + b, "ep", 128 * b, "sl%d" % t, 0, 128, False, True)
-        for b in range(4):
-            scp(rg("dl", b, 256, 4), rg("ps", 1024 + 512 * b, 1024 + 512 * b + 64))
 
     def decide(t):
         n2, v2 = q0("mi", 2 * t, 2 * t + 1), q0("mi", 2 * t + 1, 2 * t + 2)
@@ -410,13 +431,13 @@ def rank_program(g, core, T, topo):
         ts(q0("h2", 4, 11), THR, n2, Op.is_le)
         ts(WIN, v2, OWNV, Op.is_ge if grp else Op.is_gt)
         scan(q0("kb", 19, 65), q0("hw", 0, 46), q0("h2", 0, 46), 0.0, mul, add)
-        ts(DCOL, WIN, 32.0, mul, C0, add)
+        fma(WC, WIN, 128.0, PF)
+        fma(DCOL, WIN, 32.0, C0)
+        for b in range(4):
+            scp(rg("dl", b, 256, 4), rg("ps", 1024 + 512 * b, 1024 + 512 * b + 64))
         turn(q0("kt"), q0("kb", 32, 64))
-        ts(WC, WIN, 128.0, mul, PF, add)
         ts(q0("eq"), q0("kt"), KEY, Op.is_equal)
-        ts(MISS, KEY, float(N), Op.is_lt)
         red(CNT, q0("eq"), add)
-        ts(DM, KEY, float(N), Op.is_lt, DCOL, mul)
 
     def step(t):
         o, i, w, f = rg("xt", 128 * t + 128, 128 * t + 256), rg("xt", 128 * t, 128 * t + 128), rg("dl"), rg("of")
@@ -428,24 +449,25 @@ def rank_program(g, core, T, topo):
 
     def move(t):
         ts(q0("xb", 0, 32), q0("mu"), CNT, Op.is_gt, WC, mul)
-        ts(FET, CNT, CAPP + 0.5, Op.is_lt, MISS, mul)
-        later = fold("xb", "k4")
-        ts(OF4, HOT, FET, mul)
-        later()
-        ts(DN, q0("mi", 2 * t, 2 * t + 1), OWNN, sub, WIN, mul)
+        fold("xb", "k4")()
         spread("of", q0("xb", 67, 96, 4), P4)
-        ts(T4, AN, OWNN, sub, DN, sub)
+        ts(DM, KEY, float(N), Op.is_lt, DCOL, mul)
+        ts(MISS, KEY, float(N), Op.is_lt)
         step(t)
 
     def slots(t):
         ts(q0("xd", 0, 32), q0("mt"), CNT, Op.is_gt, DM, mul)
-        tt(T5, T4, OF4, mul)
+        ts(FET, CNT, CAPP + 0.5, Op.is_lt, MISS, mul)
         later = fold("xd", "k16")
-        tt(AN, AN, T5, sub)
+        ts(DN, q0("mi", 2 * t, 2 * t + 1), OWNN, sub, WIN, mul)
         later()
+        ts(OF4, HOT, FET, mul)
         changed()
+        ts(T4, AN, OWNN, sub, DN, sub)
         tt(L9, L8, BASEP, add)
+        tt(T5, T4, OF4, mul)
         spread("ol", L9, 64.0)
+        tt(AN, AN, T5, sub)
         pick("sl%d" % (t + 1), 64, "sl%d" % t, 0, 192, "ol")
 
     def finish(t):
@@ -457,29 +479,30 @@ def rank_program(g, core, T, topo):
         sums[1]()
         changed()
         ts(DN, q0("mi", 2 * t, 2 * t + 1), OWNN, sub, WIN, mul)
-        ts(FET, CNT, CAPP + 0.5, Op.is_lt, MISS, mul)
         tt(L9, L8, BASEP, add)
-        ts(OF4, HOT, FET, mul)
+        ts(FET, CNT, CAPP + 0.5, Op.is_lt, MISS, mul)
         spread("ol", L9, 64.0)
         ts(T4, AN, OWNN, sub, DN, sub)
         pick(last, 64, "sl%d" % t, 0, 192, "ol")
         store("y", T.oc[:, :], rg(last + "c", 64, 192), u8(rg(last + "c", 64, 192)))
         spread("of", q0("xb", 67, 96, 4), P4)
-        tt(T5, T4, OF4, mul)
+        ts(OF4, HOT, FET, mul)
         products(t)
         store("s", T.y[:, 256 * t:256 * t + 256], rg("ys", 256 * t, 256 * t + 256))
         step(t)
-        tt(AN, AN, T5, sub)
+        tt(T5, T4, OF4, mul)
         cp(rg("pxs"), rg("xt", 128 * R, 128 * R + 128))
-        turn(q0("ant"), q0("anb"))
+        tt(AN, AN, T5, sub)
         for a in range(4):
             store("y", T.osc[4 * a:4 * a + 4, :], rg(last + "s", 64, 192, 1, 32 * a, 32 * a + 4))
-        store("y", T.px[:, :], rg("pxs"))
-        store("s", T.an[:, :], rg("ant", 0, 32, 1, 0, 4))
+        store("s", T.px[:, :], rg("pxs"))
+        turn(q0("ant"), q0("anb"))
+        store("y", T.an[:, :], rg("ant", 0, 32, 1, 0, 4))
 
     for t in range(R):
         worst(t)
         if t == 0:
+            quant("ep", 0, 512, rg("ct"))
             wait("y", "set%d" % (near[0] % G), 2 * len(topo.engines(T.cores[near[0]], core)))
             load("y", rg("wt"), T.w[:, :], "lw")
         score(t)
@@ -495,6 +518,8 @@ def rank_program(g, core, T, topo):
             send_e(t + 1)
             slots(t)
         else:
+            ts(DM, KEY, float(N), Op.is_lt, DCOL, mul)
+            ts(MISS, KEY, float(N), Op.is_lt)
             finish(t)
     for q in "vstg":
         wait("g", q + "n", count[q])

@@ -4,29 +4,29 @@ from concourse.mybir import dt, AluOpType, AxisListType, ActivationFunctionType
 N, A, M, CAPP, R, O = 8, 320, 32, 3, 3, 2
 CORES = 256
 G = N // 2
-NREL = 4
 PW = A // 2
-BIG = 1.0e6
+BIG, HOLD = 1.0e6, 4096.0
+XW = 512
 CODE, F32, BF, I32, U8, U16 = "float8_e4m3fn_x4", "float32", "bfloat16", "int32", "uint8", "uint16"
 
 SCRATCH = {}
-for _n, _w in (("qd", A), ("at", G * A), ("rl", PW), ("es", 128 + 160 * R), ("fa", 64 * R + 128), ("ep", 512), ("en", 512),
-               ("wq", 128 * O), ("ca0", M), ("ca1", M), ("ca2", M), ("sl0", 192), ("sl1", 192), ("sl2", 192), ("sl3", 192)):
+for _n, _w in (("qd", A), ("at", G * A), ("rl", A), ("es0", 288), ("es1", 288), ("es2", 288), ("fa", 128 + 2 * M * R), ("ep", 512), ("en", 512),
+               ("wq", 128 * O), ("ca", M * R), ("sl0", 192), ("sl1", 192), ("sl2", 192), ("sl3", 128)):
     SCRATCH[_n + "c"] = ("sbuf", [128, _w], CODE)
     SCRATCH[_n + "s"] = ("sbuf", [128, _w], U8)
-for _n, _w, _d in (("dtile", 4 * A, BF), ("xt", 128 * (R + 1), BF), ("bt", 128, BF), ("wt", 512 * O, BF), ("et", 512, BF), ("zt", 512, BF),
-                   ("ct", 2048, BF), ("zf", A, F32), ("rm", 2 * A, F32), ("sg", 2 * A, F32), ("ys", R * O * 128, F32), ("pxs", 128, F32),
-                   ("idt", 128, BF), ("dl", 264, F32), ("io1", 128, I32), ("io2", 32, I32), ("io3", 32, I32), ("ia", 128, I32), ("ib", 128, I32),
-                   ("acti", 8, I32), ("m1", 32, F32), ("mt", 32, F32), ("mu", 32, F32), ("k16", 32, F32), ("k4", 32, F32),
-                   ("dg", 128, F32), ("pen", 40, F32), ("cs", 48, F32), ("kb", 72, F32), ("hw", 48, F32), ("kt", 32, F32), ("eq", 32, F32),
-                   ("xa", 96, F32), ("xb", 96, F32), ("xc", 96, F32), ("xd", 96, F32), ("sc", 384, F32),
-                   ("sm", 96, F32), ("h1", 12, F32), ("h2", 48, F32), ("anb", 32, F32), ("ant", 32, F32),
-                   ("mo", 8 * R, F32), ("mi", 2 * R, F32),
-                   ("oc2", 2, U16), ("oo", 2, U16), ("oa", 2, U16), ("of", 8, U16), ("ol", 8, U16)):
+for _n, _w, _d in (("dtile", 4 * A, BF), ("xt", 128, BF), ("xp", XW * R, BF), ("bt", 128, BF), ("wt", 512 * O, BF), ("et", 512, BF), ("zt", 512, BF),
+                   ("ct", 2048, BF), ("rm", 2 * A, F32), ("sg", 2 * A, F32), ("ys", 768, F32), ("pxs", 128, F32),
+                   ("idt", 128, BF), ("io1", 128, I32), ("io2", 32, I32), ("io3", 32, I32), ("ia", 32, I32), ("ib", 128, I32),
+                   ("acti", 8, I32), ("mz", 32, F32), ("xe", 64, F32), ("mn", 32, F32), ("mu", 32, F32), ("k16", 32, F32),
+                   ("dg", 128, F32), ("pen", 40, F32), ("cs", 48, F32), ("kb", 100, F32), ("hw", 72, F32), ("hv", 16, F32), ("kt", 32, F32),
+                   ("eq", 64, F32), ("da", 64, F32), ("za", 64, F32), ("ml", 72, F32),
+                   ("xa", 192, F32), ("xb", 112, F32), ("xd", 96, F32), ("sc", 384, F32), ("tb", 32, F32),
+                   ("sm", 96, F32), ("h1", 16, F32), ("h2", 72, F32), ("anb", 32, F32), ("ant", 32, F32),
+                   ("mo", 4 * R, F32), ("mi", 4 * R, F32), ("oa", 4, U16), ("oo", 2, U16), ("oe", 2, U16), ("ol", 10, U16)):
     SCRATCH[_n] = ("sbuf", [128, _w], _d)
 SCRATCH["ps"] = ("psum", [128, 4096], F32)
 
-SEMAPHORES = (["vn", "sn", "tn", "gn", "sent", "ld0", "ld1", "lx", "lb", "la", "lw", "sty", "sts", "rc", "rs"]
+SEMAPHORES = (["vn", "sn", "tn", "gn", "sent", "ld0", "ld1", "lx", "lb", "la", "la2", "lw", "sty", "sts", "rs", "rc"]
               + ["set%d" % k for k in range(G)]
               + ["%s%d" % (s, t) for s in ("ee", "me", "cc", "cz") for t in range(R)])
 
@@ -60,7 +60,7 @@ def ways(T, topo, r):
         same = [u for u in able if topo.die(u) == topo.die(c)]
         other = [u for u in able if u not in same]
         away.append((same, other)[sorted([r] + near).index(r)][0])
-    return near, far, away + home[:2]
+    return near, far, [away, home[:2]]
 
 
 def share(engines, n, j):
@@ -68,11 +68,10 @@ def share(engines, n, j):
     return engines[j * w:j * w + w]
 
 
-def job(T, topo, r, j):
-    near, far, relays = ways(T, topo, r)
-    off = topo.engines(T.cores[r], relays[0])
-    use = off if j < 2 else [e for e in topo.engines(T.cores[r], relays[j]) if e not in off]
-    return j // 2, far[j % 2], share(use, 2, j % 2)
+def feed(T, topo, r, w, j):
+    relays = ways(T, topo, r)[2]
+    off = topo.engines(T.cores[r], relays[0][0])
+    return share(off if w == 0 else [e for e in topo.engines(T.cores[r], relays[w][j]) if e not in off], 2, j)
 
 
 def send(g, T, topo, core, moves):
@@ -89,32 +88,75 @@ def send(g, T, topo, core, moves):
     return sum(len(m[4]) for m in moves)
 
 
-def relay_program(g, core, T, topo, r, j):
-    half, to, got = job(T, topo, r, j)
-    lo = (r % G) * A + half * PW
-    n = 0
-    for sem, src, dst in (("rs", T.rls[:], T.ats[:, lo:lo + PW]), ("rc", T.rlc[:].bitcast(dt.uint8), T.atc[:, lo:lo + PW].bitcast(dt.uint8))):
-        g.wait_ge(T.sem[sem], len(got))
-        n += send(g, T, topo, core, [(T.cores[to], dst, src, "set%d" % (r % G), topo.engines(core, T.cores[to]))])
+def relay_program(g, core, T, topo, r, w, j):
+    to = T.cores[ways(T, topo, r)[1][j]]
+    c0, base, n = w * PW, (r % G) * A + w * PW, 0
+    for x in "sc":
+        src, dst = T["rl" + x][:, c0:c0 + PW], T["at" + x][:, base:base + PW]
+        if x == "c":
+            src, dst = src.bitcast(dt.uint8), dst.bitcast(dt.uint8)
+        g.wait_ge(T.sem["r" + x], len(feed(T, topo, r, w, j)))
+        n += send(g, T, topo, core, [(to, dst, src, "set%d" % (r % G), topo.engines(core, to))])
     g.wait_ge(T.sem.sent, n)
+
+
+CYC, WAKE = 1.04e-3, 0.09
+
+
+def order(nodes):
+    after = [[] for _ in nodes]
+    for j, n in enumerate(nodes):
+        for i in n["deps"]:
+            after[i].append(j)
+    left = [0.0] * len(nodes)
+    for i in range(len(nodes) - 1, -1, -1):
+        left[i] = max([nodes[i]["lat"]] + [left[j] + (nodes[i]["lat"] + WAKE if nodes[j]["deps"][i] else nodes[i]["hold"]) for j in after[i]])
+    miss = [len(n["deps"]) for n in nodes]
+    ready = [i for i in range(len(nodes)) if not miss[i]]
+    done, free, out, end = {}, {}, [], max(left)
+    while ready:
+        est = {}
+        for i in ready:
+            n = nodes[i]
+            est[i] = max([free.get(n["q"], 0.0) if n["q"] != "r" else 0.0] + [done[d][0] + WAKE if w else done[d][1] for d, w in n["deps"].items()])
+        first = min(ready, key=lambda i: (est[i], -left[i]))
+        q = nodes[first]["q"]
+        mine = [i for i in ready if nodes[i]["q"] == q]
+        pick = max([i for i in mine if est[i] <= est[first] + 0.02], key=lambda i: left[i])
+        if q != "r":
+            stop = est[pick] + nodes[pick]["hold"]
+            urgent = [i for i in mine if left[i] > left[pick] and est[i] < stop and stop + left[i] > end - 1.0]
+            if urgent:
+                pick = min(urgent, key=lambda i: (est[i], -left[i]))
+        n = nodes[pick]
+        free[q] = est[pick] + n["hold"]
+        done[pick] = (est[pick] + n["lat"], est[pick])
+        end = max(end, est[pick] + left[pick])
+        ready.remove(pick)
+        out.append(pick)
+        for j in after[pick]:
+            miss[j] -= 1
+            if not miss[j]:
+                ready.append(j)
+    return out
 
 
 def rank_program(g, core, T, topo):
     rank = T.rank_of(core)
     if rank is None:
         for r in range(N):
-            relays = ways(T, topo, r)[2]
-            if core in relays:
-                relay_program(g, core, T, topo, r, relays.index(core))
+            for w, row in enumerate(ways(T, topo, r)[2]):
+                if core in row:
+                    relay_program(g, core, T, topo, r, w, row.index(core))
         return
     k, grp = rank % G, rank // G
     near, far, relays = ways(T, topo, rank)
     mate = T.cores[partners(T, topo)[rank]]
     em = topo.engines(core, mate)
+    ne = len(topo.engines(mate, core))
     Q = {"v": g.vector, "s": g.scalar, "t": g.tensor, "g": g, "y": g.sync}
-    seen = {q: {} for q in Q}
-    count = {"v": 0, "s": 0, "t": 0, "g": 0, "sent": 0, "sty": 0, "sts": 0}
-    log = {}
+    nodes, log, last = [], {}, {}
+    sent = [0]
     add, sub, mul, Op, Fn = AluOpType.add, AluOpType.subtract, AluOpType.mult, AluOpType, ActivationFunctionType
 
     def rg(name, c0=0, c1=None, step=1, p0=0, p1=128):
@@ -126,10 +168,19 @@ def rank_program(g, core, T, topo):
     def h0(name, c0=0, c1=None, step=1):
         return rg(name, c0, c1, step, 0, 64)
 
+    def half(r, h):
+        return r[:1] + (64 * h, 64 * h + 64) + r[3:]
+
+    def run32(r, a):
+        return r[:1] + (32 * a, 32 * a + 32) + r[3:]
+
     def ap(r):
         if not isinstance(r, tuple):
             return r
         return T[r[0]][r[1]:r[2], r[3]:r[4]:r[5]] if r[5] != 1 else T[r[0]][r[1]:r[2], r[3]:r[4]]
+
+    def wide(r):
+        return len(range(r[3], r[4], r[5]))
 
     def meet(a, b):
         if a[0] == "ps":
@@ -138,144 +189,160 @@ def rank_program(g, core, T, topo):
             return False
         return not (a[5] == b[5] and (a[3] - b[3]) % a[5])
 
-    def wait(q, sem, n):
-        if seen[q].get(sem, 0) < n:
-            Q[q].wait_ge(T.sem[sem], n)
-            seen[q][sem] = n
+    def node(q, outs, ins, call, hold, lat=None, sem=None, n=0, behind=(), chain=None):
+        deps = {}
+        uses = [(r, True) for r in outs] + [(r, False) for r in ins if isinstance(r, tuple)]
+        for r, w in uses:
+            for r2, w2, j in log.get(r[0], ()):
+                if meet(r, r2):
+                    if r[0] == "ps":
+                        if nodes[j]["q"] != q:
+                            deps[j] = True
+                        elif q == "t":
+                            deps.setdefault(j, False)
+                    elif w or w2:
+                        deps[j] = True
+        for j in behind:
+            deps[j] = True
+        if chain:
+            if chain in last:
+                deps.setdefault(last[chain], False)
+            last[chain] = len(nodes)
+        for r, w in uses:
+            log.setdefault(r[0], []).append((r, w, len(nodes)))
+        nodes.append({"q": q, "deps": deps, "call": call, "hold": hold, "lat": hold if lat is None else lat, "sem": sem, "n": n})
+        return len(nodes) - 1
 
-    def before(q, outs, ins):
-        need = {}
-        for r, w in [(r, True) for r in outs] + [(r, False) for r in ins if isinstance(r, tuple)]:
-            for r2, w2, q2, sem, n in log.get(r[0], ()):
-                if meet(r, r2) and ((q != q2) if r[0] == "ps" else (w or w2)):
-                    need[sem] = max(need.get(sem, 0), n)
-        for sem in sorted(need):
-            wait(q, sem, need[sem])
+    def later(j, d):
+        nodes[j]["deps"].setdefault(d, False)
 
-    def note(q, outs, ins, sem, n):
-        for r, w in [(r, True) for r in outs] + [(r, False) for r in ins if isinstance(r, tuple)]:
-            log.setdefault(r[0], []).append((r, w, q, sem, n))
+    def run(q, outs, ins, call, cyc=64):
+        return node(q, outs, ins, call, max(64, cyc) * CYC, chain="g" if q == "g" else None)
 
-    def run(q, outs, ins, call):
-        before(q, outs, ins)
-        count[q] += 1
-        call().then_inc(T.sem[q + "n"], 1)
-        note(q, outs, ins, q + "n", count[q])
+    def load(q, out, src, sem, lat, behind=()):
+        return node(q, [out], [], lambda: Q[q].dma_start(ap(out), src).then_inc(T.sem[sem], 16), 0.06, lat, sem, 16, behind, "load" + q)
 
-    def load(q, out, src, sem, n=16):
-        Q[q].dma_start(ap(out), src).then_inc(T.sem[sem], 16)
-        note(q, [out], [], sem, n)
-
-    def store(q, dst, src, view=None):
-        before(q, [], [src])
-        Q[q].dma_start(dst, view if view is not None else ap(src)).then_inc(T.sem["st" + q], 16)
-        count["st" + q] += 16
+    def store(q, dst, src, view=None, lat=2.0, behind=()):
+        node(q, [], [src], lambda: Q[q].dma_start(dst, view if view is not None else ap(src)).then_inc(T.sem["st" + q], 16), 0.06, lat, "st" + q, 0, behind)
 
     def post(srcs, moves):
-        before("g", [], srcs)
-        count["sent"] += send(g, T, topo, core, moves)
+        def call():
+            sent[0] += send(g, T, topo, core, moves)
+        return node("g", [], srcs, call, 0.12, 0.12, "sent", 0, (), "g")
+
+    def lands(outs, sem, n, mirror, lat):
+        j = node("r", outs, [], None, lat, lat, sem, n)
+        later(j, mirror)
+        return j
 
     def u8(r):
         return ap(r).bitcast(dt.uint8)
 
+    def view(r):
+        return u8(r) if SCRATCH[r[0]][2] == CODE else ap(r)
+
     def ts(o, i, s1, op0, s2=None, op1=None):
         if op1 is None:
-            run("v", [o], [i, s1], lambda: g.vector.tensor_scalar(ap(o), ap(i), ap(s1), None, op0))
-        else:
-            run("v", [o], [i, s1, s2], lambda: g.vector.tensor_scalar(ap(o), ap(i), ap(s1), ap(s2), op0, op1))
+            return run("v", [o], [i, s1], lambda: g.vector.tensor_scalar(ap(o), ap(i), ap(s1), None, op0), wide(o))
+        return run("v", [o], [i, s1, s2], lambda: g.vector.tensor_scalar(ap(o), ap(i), ap(s1), ap(s2), op0, op1), wide(o))
 
     def tt(o, a, b, op):
-        run("v", [o], [a, b], lambda: g.vector.tensor_tensor(ap(o), ap(a), ap(b), op))
-
-    def red(o, i, op, neg=False):
-        run("v", [o], [i], lambda: g.vector.tensor_reduce(ap(o), ap(i), AxisListType.X, op, negate=neg))
+        run("v", [o], [a, b], lambda: g.vector.tensor_tensor(ap(o), ap(a), ap(b), op), wide(o) * (1 if a[0] == "ps" else 2))
 
     def scan(o, a, b, first, op0, op1):
-        run("v", [o], [a, b], lambda: g.vector.tensor_tensor_scan(ap(o), ap(a), ap(b), first, op0, op1))
+        run("v", [o], [a, b, first], lambda: g.vector.tensor_tensor_scan(ap(o), ap(a), ap(b), ap(first), op0, op1), wide(o))
 
     def cp(o, i):
-        run("v", [o], [i], lambda: g.vector.tensor_copy(ap(o), ap(i)))
+        return run("v", [o], [i], lambda: g.vector.tensor_copy(ap(o), ap(i)), wide(o))
 
     def scp(o, i):
-        run("s", [o], [i], lambda: g.scalar.activation(ap(o), ap(i), Fn.Copy))
+        run("s", [o], [i], lambda: g.scalar.activation(ap(o), ap(i), Fn.Copy), wide(o))
 
-    def fma(o, i, scale, bias):
-        run("s", [o], [i, scale, bias], lambda: g.scalar.activation(ap(o), ap(i), Fn.Identity, bias=ap(bias), scale=ap(scale)))
+    def fma(o, i, scale, bias, fn=Fn.Identity):
+        run("s", [o], [i, scale, bias], lambda: g.scalar.activation(ap(o), ap(i), fn, bias=ap(bias), scale=ap(scale)), wide(o))
 
-    def ahead(o, i, last, n):
-        run("s", [o, n], [i], lambda: g.scalar.activation(ap(o), ap(i), Fn.Sign, bias=ap(last), scale=-1.0, accum_out=ap(n)))
+    def summed(o, i, scale, bias, n, fn):
+        run("s", [o, n], [i, bias], lambda: g.scalar.activation(ap(o), ap(i), fn, bias=ap(bias), scale=scale, accum_out=ap(n)), max(64, wide(o)) + 24)
+
+    def ahead(o, i, n):
+        summed(o, i, -1.0, i[:3] + (i[4] - 1, i[4], 1), n, Fn.Sign)
 
     def fill(o, v):
-        run("v", [o], [], lambda: g.vector.memset(ap(o), v))
+        run("v", [o], [], lambda: g.vector.memset(ap(o), v), wide(o) // (2 if SCRATCH[o[0]][2] == BF else 1))
 
     def turn(o, i):
-        run("v", [o], [i], lambda: g.vector.transpose(ap(o), ap(i)))
-
-    def fold(x, keep, rows=q0):
-        turn(rows(x, 32, 64), rows(x, 0, 32))
-        return lambda: scan(rows(x, 64, 96), rows(keep), rows(x, 32, 64), 0.0, mul, add)
+        run("v", [o], [i], lambda: g.vector.transpose(ap(o), ap(i)), wide(o))
 
     def quant(name, c0, c1, i):
         c, s = rg(name + "c", c0, c1), rg(name + "s", c0, c1)
-        run("v", [c, s], [i], lambda: g.vector.quantize_mx(ap(c), ap(s), ap(i)))
+        return run("v", [c, s], [i], lambda: g.vector.quantize_mx(ap(c), ap(s), ap(i)), 15 + 1.06 * (c1 - c0))
 
     def mm(bank, st, s0, mv, m0, n, start, stop):
         o = rg("ps", 512 * bank, 512 * bank + n)
         i = [rg(st + "c", s0, s0 + 128), rg(st + "s", s0, s0 + 128), rg(mv + "c", m0, m0 + n), rg(mv + "s", m0, m0 + n)]
-        run("t", [o], i, lambda: g.tensor.matmul_mx(ap(o), ap(i[0]), ap(i[1]), ap(i[2]), ap(i[3]), start, stop))
+        return run("t", [o], i, lambda: g.tensor.matmul_mx(ap(o), ap(i[0]), ap(i[1]), ap(i[2]), ap(i[3]), start, stop), 0.6 * (n + 16))
 
-    def pick(dst, d0, src, s0, s1, off):
-        n, f = 16 * SCRATCH[off][1][1], rg(off)
+    def gather(o, i, f):
+        run("s", [o], [i, f], lambda: g.scalar.activation(ap(o), ap(i).indirect(ap(f)), Fn.Copy), 78 + 1.5 * wide(o))
+
+    def chosen(o, i, f, b):
+        run("v", [o], [i, f, b], lambda: g.vector.tensor_tensor(ap(o), ap(i).indirect(ap(f)), ap(b), add), 60 + 1.5 * wide(o))
+
+    def minus(q, o, i, f):
+        if q == "v":
+            run("v", [o], [i, f], lambda: g.vector.tensor_scalar(ap(o), ap(i).indirect(ap(f)), -1.0, None, mul), 60 + 1.5 * wide(o))
+        else:
+            run("s", [o], [i, f], lambda: g.scalar.activation(ap(o), ap(i).indirect(ap(f)), Fn.Identity, bias=0.0, scale=-1.0), 78 + 1.5 * wide(o))
+
+    def pick(dst, d0, src, s0, s1, f):
+        n = 16 * wide(f)
         o, i = rg(dst + "c", d0, d0 + n), rg(src + "c", s0, s1)
-        run("v", [o], [i, f], lambda: g.vector.tensor_copy(ap(o).bitcast(dt.uint32), ap(i).bitcast(dt.uint32).indirect(ap(f))))
-        o2, i2 = rg(dst + "s", d0, d0 + n), rg(src + "s", s0, s1)
-        run("s", [o2], [i2, f], lambda: g.scalar.activation(ap(o2), ap(i2).indirect(ap(f)), Fn.Copy))
+        run("v", [o], [i, f], lambda: g.vector.tensor_copy(ap(o).bitcast(dt.uint32), ap(i).bitcast(dt.uint32).indirect(ap(f))), 60 + 1.5 * n)
+        gather(rg(dst + "s", d0, d0 + n), rg(src + "s", s0, s1), f)
 
-    def spread(off, src, shift=None):
-        for a in range(4):
-            o = rg(off, p0=32 * a, p1=32 * a + 32)
-            if shift is None:
-                cp(o, src)
-            else:
-                ts(o, src, shift, add)
+    def spread(off, src):
+        return [cp(rg(off, 0, wide(src), 1, 32 * a, 32 * a + 32), src) for a in range(4)]
 
+    load("y", rg("dtile", 0, 4 * PW), T.d[:, 0:4 * PW], "ld0", 0.5)
+    load("y", rg("dtile", 4 * PW, 4 * A), T.d[:, 4 * PW:4 * A], "ld1", 0.8)
+    load("y", rg("xt"), T.x[:, :], "lx", 1.0)
+    load("y", rg("bt"), T.b[:, :], "lb", 1.1)
+    load("s", rg("acti", p0=0, p1=16), T.act[:, :], "la", 2.0)
+    load("s", rg("acti", p0=16, p1=32), T.act[:, :], "la2", 2.2)
+    run("g", [rg("io1")], [], lambda: g.iota(T.io1[:], [[-1, 128]], 128, 1), 330)
+    run("g", [rg("io2")], [], lambda: g.iota(T.io2[:], [[0, 2], [1, 16]], 0, 0), 180)
+    run("g", [rg("io3")], [], lambda: g.iota(T.io3[:], [[1, 32]], 0, 0), 180)
+
+    for w in range(2):
+        quant("qd", w * PW, w * PW + PW, rg("dtile", 4 * PW * w, 4 * PW * w + 4 * PW))
+        for x in "sc":
+            src = rg("qd" + x, w * PW, w * PW + PW)
+            relayed = post([src], [(u, view(rg("rl" + x, w * PW, w * PW + PW)), view(src), "r" + x, feed(T, topo, rank, w, j)) for j, u in enumerate(relays[w])])
+    for x in "cs":
+        src = rg("qd" + x)
+        direct = post([src], [(T.cores[q], view(rg("at" + x, k * A, k * A + A)), view(src), "set%d" % k, topo.engines(core, T.cores[q])) for q in near])
+
+    def send_e(t, lat=1.3):
+        for x in "cs":
+            src = rg("es%d%s" % (t, x), 160, 192)
+            j = post([src], [(mate, view(rg("es%d%s" % (t, x), 128, 160)), view(src), "ee%d" % t, em)])
+        lands([rg("es%dc" % t, 128, 160), rg("es%ds" % t, 128, 160)], "ee%d" % t, 2 * ne, j, lat)
+
+    fill(rg("zt"), 0.0)
+    scp(rg("et", 128, 512), rg("zt", 0, 384))
+    tt(rg("et", 0, 128), rg("bt"), rg("xt"), sub)
+    quant("es0", 160, 288, rg("et"))
+    send_e(0, 6.8)
     for q in range(grp * G, grp * G + G):
         if q != rank:
             qn, qf, qr = ways(T, topo, q)
-            if rank in qn:
-                n = 2 * len(topo.engines(T.cores[q], core))
-            else:
-                n = sum(2 * len(topo.engines(u, core)) for i, u in enumerate(qr) if job(T, topo, q, i)[1] == rank)
             j = q % G
-            note("r", [rg("atc", j * A, j * A + A), rg("ats", j * A, j * A + A)], [], "set%d" % j, n)
-    ne = len(topo.engines(mate, core))
-    for t in range(R):
-        e0 = 128 + 160 * t
-        note("r", [rg("esc", e0, e0 + M), rg("ess", e0, e0 + M)], [], "ee%d" % t, 2 * ne)
-        note("r", [rg("mi", 2 * t, 2 * t + 2)], [], "me%d" % t, ne)
-        note("r", [rg("sl%dc" % t, M, 2 * M)], [], "cc%d" % t, ne)
-        note("r", [rg("sl%ds" % t, M, 2 * M)], [], "cz%d" % t, ne)
-
-    H = 2 * A
-    load("y", rg("dtile", 0, H), T.d[:, 0:H], "ld0")
-    load("y", rg("dtile", H, 2 * H), T.d[:, H:2 * H], "ld1")
-    load("y", rg("xt", 0, 128), T.x[:, :], "lx")
-    load("y", rg("bt"), T.b[:, :], "lb")
-    load("s", rg("acti", p0=0, p1=16), T.act[:, :], "la", 32)
-    load("s", rg("acti", p0=16, p1=32), T.act[:, :], "la", 32)
-    run("g", [rg("io1")], [], lambda: g.iota(T.io1[:], [[-1, 128]], 128, 1))
-    run("g", [rg("io2")], [], lambda: g.iota(T.io2[:], [[1, 32]], 0, 0))
-    run("g", [rg("io3")], [], lambda: g.iota(T.io3[:], [[0, 2], [1, 4], [0, 4]], 128, -1))
-    fill(rg("zt"), 0.0)
-    for name, n in (("et", 512), ("zf", A)):
-        scp(rg(name), rg("zt", 0, n))
-    for b in range(4):
-        scp(rg("ct", 512 * b, 512 * b + 512), rg("zt"))
-    for name in ("mo", "anb"):
-        fill(rg(name), 0.0)
-    fill(rg("dl", 256, 264), 0.0)
-    quant("es", 0, 128, rg("zt"))
-    quant("fa", 64 * R, 64 * R + 128, rg("zt"))
+            outs = [rg("atc", j * A, j * A + A), rg("ats", j * A, j * A + A)]
+            if rank in qn:
+                got = lands(outs, "set%d" % j, 2 * len(topo.engines(T.cores[q], core)), direct, 7.3)
+            else:
+                lands(outs, "set%d" % j, sum(2 * len(topo.engines(row[qf.index(rank)], core)) for row in qr), relayed, 8.0)
+    load("y", rg("wt"), T.w[:, :], "lw", 2.6, [got])
 
     def cs(c, n=1, rows=q0):
         return rows("cs", c, c + n)
@@ -283,246 +350,261 @@ def rank_program(g, core, T, topo):
     def sm(c, n=1, rows=q0):
         return rows("sm", c, c + n)
 
-    U, THR, NEG4, STEP5, BASEP, HI, PM, P4, PI, PF = cs(0), cs(1, 7), cs(8, 4), cs(32, 5, h0), cs(16, 8), cs(24), cs(25), cs(26), cs(27), cs(28)
+    NEG4, BASEP, HI, PM, PH, PI, PP, PL = cs(8, 4), cs(16, 8), cs(24), cs(25), cs(26), cs(27), cs(28), cs(29)
     P128 = q0("io1", 0, 1)
-    ts(h0("ia", 0, 32), h0("io1", 0, 32), 15, Op.bitwise_and)
-    ts(q0("ib"), q0("io1"), 31, Op.bitwise_and)
-    ts(q0("ia", 32, 64), q0("io3"), 3, Op.bitwise_and)
-    ts(h0("ia", 64, 96), h0("io2"), 15, Op.bitwise_and)
-    ts(q0("ia", 96, 128), q0("io2"), 3, Op.bitwise_and)
-    ts(q0("pen", 0, 33), q0("io1", 0, 33), 128.0, Op.is_gt, 1000.0, mul)
-    ts(U, P128, 8.0, mul, 16.0 - 8 * 128, add)
-    ts(HI, P128, 128.0 + 16, Op.is_ge)
-    ts(PI, P128, -128.0 - 64, add)
-    ts(PF, P128, 4.0, mul, -4.0 * (128 + 64), add)
-    ts(THR, q0("io2", 0, 7), float(A), mul, float(A), add)
-    ts(h0("m1"), h0("ia", 0, 32), 0.0, Op.is_equal)
-
-    jobs = [job(T, topo, rank, j) for j in range(NREL)]
-    for h in range(2):
-        quant("qd", h * PW, h * PW + PW, rg("dtile", h * H, h * H + H))
-        for x, view, sem in (("s", ap, "rs"), ("c", u8, "rc")):
-            src = rg("qd" + x, h * PW, h * PW + PW)
-            post([src], [(relays[j], view(rg("rl" + x)), view(src), sem, jobs[j][2]) for j in range(NREL) if jobs[j][0] == h])
-        if h == 0:
-            ts(q0("dg"), q0("ib"), 0.0, Op.is_gt, 1.0e29, mul)
-            ts(q0("mu"), q0("ia", 32, 64), 0.0, Op.is_equal, CAPP + 1.5, mul)
-            ts(h0("k16"), h0("ia", 64, 96), 0.0, Op.is_gt)
-            ts(q0("k4"), q0("ia", 96, 128), 0.0, Op.is_gt)
-            cp(PM, q0("ia", 0, 1))
-            ts(q0("ia", 33, 34), q0("ia", 0, 1), 3, Op.bitwise_and)
-    for x, view in (("c", u8), ("s", ap)):
-        for q in near:
-            post([rg("qd" + x)], [(T.cores[q], view(rg("at" + x, k * A, k * A + A)), view(rg("qd" + x)), "set%d" % k, topo.engines(core, T.cores[q]))])
-
-    def send_e(t):
-        e0 = 128 + 160 * t
-        tt(rg("et", 0, 128), rg("bt"), rg("xt", 128 * t, 128 * t + 128), sub)
-        quant("es", e0 + M, e0 + 160, rg("et"))
-        for x, view in (("c", u8), ("s", ap)):
-            src = rg("es" + x, e0 + M, e0 + 2 * M)
-            post([src], [(mate, view(rg("es" + x, e0, e0 + M)), view(src), "ee%d" % t, em)])
-
-    def tile(v):
+    own0 = float((2 * grp - 1) * G * A)
+    quant("at", k * A, k * A + A, rg("dtile"))
+    for t in range(R):
+        quant("es%d" % t, 0, 128, rg("zt"))
+    quant("fa", 0, 128, rg("zt"))
+    for b in range(4):
+        for c in range(2):
+            fma(rg("xp", 128 * b + 32 * c, 128 * b + 32 * c + 32), rg("xt", b, 128, 4), -1.0, 0.0)
+    ts(rg("idt"), rg("io1"), 128.0, Op.is_equal)
+    for b in range(4):
+        scp(rg("ct", 512 * b, 512 * b + 512), rg("zt"))
+    for name, v in (("ep", 0.25), ("en", -0.25)):
         for b in range(4):
             fma(rg("ct", 512 * b + b, 512 * b + 512, 4), rg("idt"), v, 0.0)
-
-    quant("at", k * A, k * A + A, rg("dtile"))
-    ts(rg("idt"), rg("io1"), 128.0, Op.is_equal)
-    send_e(0)
-    tile(-0.25)
-    ts(q0("mt"), q0("m1"), CAPP + 1.5, mul, -1.0, add)
-    ts(q0("mu"), q0("mu"), -1.0, add)
-    ts(BASEP, q0("io2", 0, 8), 16.0, mul, PM, add)
-    ts(NEG4, q0("io2", 0, 4), -32.0, mul, PI, sub)
-    ts(P4, q0("ia", 33, 34), 256.0, add)
-    ts(NEG4, NEG4, -64.0, add)
+        for b in range(0, 4, 2):
+            quant(name, 128 * b, 128 * b + 256, rg("ct", 512 * b, 512 * b + 1024))
+    fill(rg("mo"), 0.0)
+    fill(q0("anb"), 0.0)
+    ts(rg("ia"), rg("io1", 0, 32), 15, Op.bitwise_and)
+    ts(q0("ib"), q0("io1"), 31, Op.bitwise_and)
+    ts(q0("pen", 0, 33), q0("io1", 0, 33), 128.0, Op.is_gt, 1000.0, mul)
     fill(q0("hw"), 1.0)
-    cp(q0("h2", 13, 14), q0("pen", 0, 1))
-    tt(q0("h2", 14, 46), q0("pen", 1, 33), q0("pen", 0, 32), sub)
-    fill(cs(32, 4, h0), float(A))
-    fill(cs(36, 1, h0), float(G * A * grp))
-    fill(sm(44, 1, h0), 4 * BIG)
+    fill(q0("hw", 0, 16, 2), -1.0)
+    ts(q0("hw", 16, 17), P128, 8.0, mul, 16.0 - 8 * 128, add)
+    cp(q0("hv", 0, 15), q0("hw", 0, 30, 2))
+    ts(HI, P128, 128.0 + 16, Op.is_ge)
+    cp(PI, P128)
+    ts(PP, P128, -128.0, add)
+    ts(q0("tb", 8, 15), q0("io3", 0, 7), float(A), mul, float(A - G * A * (1 - grp)), add)
+    ts(rg("mz"), rg("ia"), 0.0, Op.is_gt, -BIG, mul)
+    ts(q0("mn"), q0("ia"), 0.0, Op.is_equal, -1.0, mul)
+    ts(q0("mu"), q0("mz"), -1.0, mul, 500.0, add)
+    ts(q0("dg"), q0("ib"), 0.0, Op.is_gt, 1.0e29, mul)
+    ts(q0("k16"), q0("io2"), 0.0, Op.is_gt)
+    cp(PM, q0("ia", 0, 1))
+    ts(PH, q0("ia", 0, 1), 16.0, add, 1.0 / 16, mul)
+    ts(PL, q0("ia", 0, 1), 1.0 / 16, mul)
+    fill(q0("eq", 32, 64), 0.0)
+    fill(q0("da"), BIG)
+    fill(q0("xb", 64, 65), 0.0)
+    ts(q0("ml", 36, 53), q0("io3", 0, 17), PM, Op.is_equal, -HOLD, mul)
+    ts(q0("ml", 54, 71), q0("io3", 0, 17), -1.0, add, PM, Op.is_equal)
+    for h in range(2):
+        ts(sm(10 + h), PM, HOLD + 16 * h, add)
+        ts(q0("ml", 17 * h, 17 * h + 17), q0("ml", 54, 71), sm(10 + h), mul)
+        tt(q0("ml", 17 * h, 17 * h + 17), q0("ml", 17 * h, 17 * h + 17), q0("ml", 36, 53), add)
+    ts(BASEP, q0("io3", 0, 8), 16.0, mul, PM, add)
+    ts(NEG4, q0("io3", 0, 4), -32.0, mul, PP, sub)
+    cp(q0("h2", 32, 33), q0("pen", 0, 1))
+    tt(q0("h2", 33, 65), q0("pen", 1, 33), q0("pen", 0, 32), sub)
+    ts(half(rg("mz"), 1), half(rg("mz"), 1), -BIG, add)
 
-    AN = q0("anb", 0, 4)
+    AN, AN1 = q0("tb", 1, 8, 2), q0("tb", 0, 8, 2)
+
+    def table():
+        fma(AN1, AN, 1.0, 1.0)
+        fma(q0("tb", 16, 31), q0("tb", 0, 15), 1.0, BIG)
+
     spread("ol", q0("acti"))
-    pick("sl0", 64, "at", k * A, k * A + A, "ol")
+    pick("sl0", 0, "at", k * A, k * A + A, rg("ol", 0, 8))
     tt(sm(0, 4), q0("acti", 1, 8, 2), q0("acti", 0, 8, 2), sub)
-    ts(sm(4, 4), sm(0, 4), HI, mul, float(A * rank), add)
+    ts(sm(4, 4), sm(0, 4), HI, mul, A * k + own0, add)
     tt(AN, sm(4, 4), q0("acti", 0, 8, 2), add)
-    quant("en", 0, 512, rg("ct"))
-    tile(0.25)
+    table()
 
     NPOS, HOT, C0 = sm(20), sm(21, 4), sm(25)
-    V4, PEN4, KEY5 = sm(28, 4, h0), sm(36, 4, h0), sm(40, 5, h0)
-    OWNN, OWNV, DCOL, CNT, DM, WC = sm(46), sm(47), sm(52), sm(53), sm(54), sm(55)
-    DN, MISS, FET, OF4, T4, T5, L8, L9 = sm(60), sm(61), sm(62), sm(64, 4), sm(68, 4), sm(72, 4), sm(76, 8), sm(84, 8)
-    KEY, NKEY, KEY1, WIN = q0("kb", 64, 65), q0("h2", 11, 12), q0("h2", 12, 13), q0("hw", 12, 13)
+    CA, POS, K2, PO2, FC = [sm(c, 1, rg) for c in range(26, 31)]
+    OWNN, OWNV, N1, N2, DCOL, DM = sm(46), sm(47), sm(48), sm(49), sm(52), sm(54)
+    ROOM, WC = q0("za", 31, 32), q0("da", 32, 33)
+    DN, FN, FET, OF4, T4, T5, L8, L9 = sm(60), sm(61), sm(62), sm(64, 4), sm(68, 4), sm(72, 4), sm(76, 8), sm(84, 8)
+    KEY, NKEY, KEY1, WIN = q0("kb", 96, 97), q0("h2", 30, 31), q0("h2", 31, 32), q0("hw", 31, 32)
 
     def worst(t):
-        mm(6, "es", 128 + 160 * t + M, "sl%d" % t, 64, 128, True, True)
+        mm(6, "es%d" % t, 160, "sl%d" % t, 0, 128, True, True)
         tt(q0("sc", 0, 128), q0("ps", 3072, 3200), q0("dg"), add)
         scan(q0("sc", 128, 256), q0("sc", 0, 128), q0("sc", 0, 128), 5.0e29, Op.min, Op.min)
-        ahead(q0("sc", 256, 384), q0("sc", 128, 256), q0("sc", 255, 256), NPOS)
+        ahead(q0("sc", 256, 384), q0("sc", 128, 256), NPOS)
         fma(C0, NPOS, 1.0, PI)
+        fma(q0("xe", 0, 32), q0("mn"), NPOS, 0.0)
+        turn(q0("xe", 32, 64), q0("xe", 0, 32))
+        scan(q0("xa", 160, 192), q0("k16"), q0("xe", 32, 64), 0.0, mul, add)
+        ts(HOT, NEG4, NPOS, Op.is_equal)
 
-    def products(t):
+    def products(t, behind=()):
         for o in range(O):
-            mm(o, "wq", 128 * o, "sl%d" % (t + 1), 64, 128, True, True)
-        for o in range(O):
-            scp(rg("ys", (t * O + o) * 128, (t * O + o + 1) * 128), rg("ps", 512 * o, 512 * o + 128))
+            j = mm(2 + o, "wq", 128 * o, "sl%d" % (t + 1), 0, 128, True, True)
+            if behind:
+                later(j, behind[0])
+            (cp if o and t == R - 1 else scp)(rg("ys", 256 * t + 128 * o, 256 * t + 128 * o + 128), rg("ps", 512 * (2 + o), 512 * (2 + o) + 128))
+        store("y", T.y[:, 256 * t:256 * t + 256], rg("ys", 256 * t, 256 * t + 256), lat=2.3, behind=behind[1:])
 
     def score(t):
-        e0 = 128 + 160 * t
-        order = (k % 2, 1 - k % 2)
-        for c in order:
-            mm(c, "es", e0, "at", c * A, A, True, False)
-            mm(c, "es", e0 - 64, "at", (2 + c) * A, A, False, True)
-        for c in order:
-            u = 1 - c
-            o = rg("rm", u * A, u * A + A)
-            scan(o, rg("ps", 512 * c, 512 * c + A), rg("zf"), -1.0e29, Op.max, add)
-            ahead(rg("sg", u * A, u * A + A), o, rg("rm", u * A + A - 1, u * A + A), rg("sm", 26 + u, 27 + u))
+        es = "es%d" % t
+        CB, KK = rg("mo", 4 * t, 4 * t + 1), rg("mo", 4 * t + 2, 4 * t + 3)
+        L0, L1 = rg("rm", A - 1, A), rg("rm", 2 * A - 1, 2 * A)
+        lo, hi = half(L1, 0), half(L1, 1)
+        for c in range(2):
+            mm(c, es, 128, "at", c * A, A, True, False)
+            mm(c, es, 64, "at", (2 + c) * A, A, False, True)
+            o = rg("rm", c * A, c * A + A)
+            scan(o, rg("ps", 512 * c, 512 * c + A), rg("zt", 0, A), L0 if c else -1.0e29, Op.max, add)
+            ahead(rg("sg", c * A, c * A + A), o, (CA, CB)[c])
+        top = h0("mo", 4 * t + 1, 4 * t + 2)
+        ts(half(FC, 0), hi, lo, Op.is_gt, -BIG, mul)
+        ts(half(FC, 1), hi, lo, Op.is_gt, BIG + 2 * A, mul)
+        ts(K2, L0, L1, Op.is_lt, float(A), mul)
+        ts(KK, K2, CA, Op.max, FC, add)
+        ts(top, hi, lo, Op.max)
+        for h in range(2):
+            ts(h0("xa", 32 * h, 32 * h + 32), half(rg("mz"), h), half(KK, h), add, half(CB, h), add)
+        fma(POS, CB, 1.0, KK)
+        src = rg("mo", 4 * t, 4 * t + 3)
+        j = post([src], [(mate, ap(rg("mi", 4 * t, 4 * t + 3)), ap(src), "me%d" % t, em)])
+        lands([rg("mi", 4 * t, 4 * t + 3)], "me%d" % t, ne, j, 1.8)
+        turn(h0("xa", 64, 128), h0("xa", 0, 64))
+        for h in range(2):
+            scan(h0("xa", 128 + 16 * h, 144 + 16 * h), h0("xa", 64 + 16 * h, 80 + 16 * h), h0("xa", 96 + 16 * h, 112 + 16 * h), 0.0, Op.max, Op.max)
+        spread("oa", q0("xa", 143, 192, 16))
+        pick("ca", M * t, "at", 0, G * A, rg("oa", 0, 2))
+        for x, sem, lat in (("c", "cc", 1.6), ("s", "cz", 1.8)):
+            src, dst = rg("ca" + x, M * t, M * t + M), rg("sl%d%s" % (t, x), 160, 192)
+            j = post([src], [(mate, view(dst), view(src), "%s%d" % (sem, t), em)])
+            came = lands([dst], "%s%d" % (sem, t), ne, j, lat)
         if t:
-            products(t - 1)
-        num, top = h0("mo", 8 * t + 4, 8 * t + 5), h0("mo", 8 * t + 5, 8 * t + 6)
-        cp(sm(30, 2, h0), h0("rm", A - 1, 2 * A, A))
-        cp(sm(28, 2, h0), rg("rm", A - 1, 2 * A, A, 64, 128))
-        ts(q0("xa", 0, 32), q0("m1"), NPOS, mul, -1.0, mul)
-        red(top, V4, Op.max)
-        after = fold("xa", "k16")
-        ts(PEN4, V4, top, Op.is_lt, BIG, mul)
-        after()
-        tt(sm(42, 2, h0), sm(26, 2, h0), sm(38, 2, h0), add)
-        tt(sm(40, 2, h0), rg("sm", 26, 28, 1, 64, 128), sm(36, 2, h0), add)
-        ts(HOT, NEG4, NPOS, Op.is_equal)
-        scan(h0("mo", 8 * t, 8 * t + 5), STEP5, KEY5, BIG, add, Op.min)
-        src = rg("mo", 8 * t + 4, 8 * t + 6)
-        post([src], [(mate, ap(rg("mi", 2 * t, 2 * t + 2)), ap(src), "me%d" % t, em)])
-        ts(h0("xc", 0, 32), h0("m1"), num, mul)
-        cp(sm(46, 2), rg("mo", 8 * t + 4, 8 * t + 6, 1, 32, 64))
-        later = fold("xc", "k16", h0)
-        ts(q0("h1", 0, 4), AN, OWNN, Op.is_equal, U, mul)
-        later()
-        ts(q0("h1", 4, 11), THR, OWNN, Op.is_le)
-        spread("oc2", q0("xc", 79, 96, 16), float(-G * A * grp))
-        red(NKEY, q0("h1", 0, 11), add, True)
-        pick("ca%d" % t, 0, "at", 0, G * A, "oc2")
-        for x, view, sem in (("c", u8, "cc"), ("s", ap, "cz")):
-            src = rg("ca%d%s" % (t, x))
-            post([src], [(mate, view(rg("sl%d%s" % (t, x), M, 2 * M)), view(src), "%s%d" % (sem, t), em)])
-
-    def prepare(t):
-        f0 = 64 * (R - 1 - t)
-        fma(KEY1, NKEY, -1.0, 0.0)
-        spread("oa", q0("xa", 79, 96, 16))
-        spread("oo", rg("xc", 79, 96, 16, 32, 64), float(-G * A * grp))
-        pick("fa", f0, "sl%d" % t, 64, 192, "oa")
-        pick("fa", f0 + M, "sl%d" % t, 64, 192, "oa")
-        pick("sl%d" % t, 0, "at", 0, G * A, "oo")
-        for b in range(4):
-            mm(2 + b, "en", 128 * b, "fa", f0, 128, True, False)
-        for b in range(4):
-            mm(2 + b, "ep", 128 * b, "sl%d" % t, 0, 128, False, True)
+            products(t - 1, [j, came])
+        else:
+            later(quant("wq", 0, 128 * O, rg("wt")), j)
+        ts(N1, run32(POS, 3), -BIG, add, run32(POS, 1), Op.max)
+        fma(OWNN, N1, 1.0, own0)
+        cp(OWNV, run32(top, 1))
+        ts(q0("h1", 0, 15), q0("tb", 0, 15), OWNN, Op.is_le)
+        scan(q0("h2", 17, 32), q0("hv", 0, 15), q0("h1", 0, 15), 0.0, mul, add)
+        fma(NKEY, KEY1, -1.0, 0.0)
+        for c in range(2):
+            pick("fa", 128 + M * (2 * t + c), "sl%d" % t, 0, 128, rg("oa", 2, 4))
 
     def decide(t):
-        n2, v2 = q0("mi", 2 * t, 2 * t + 1), q0("mi", 2 * t + 1, 2 * t + 2)
-        ts(q0("h2", 0, 4), AN, n2, Op.is_equal, U, mul)
-        ts(q0("h2", 4, 11), THR, n2, Op.is_le)
-        ts(WIN, v2, OWNV, Op.is_ge if grp else Op.is_gt)
-        scan(q0("kb", 19, 65), q0("hw", 0, 46), q0("h2", 0, 46), 0.0, mul, add)
-        fma(WC, WIN, 128.0, PF)
+        cb, v2, kk = [rg("mi", 4 * t + c, 4 * t + c + 1) for c in range(3)]
+        ts(q0("h2", 0, 30, 2), q0("tb", 0, 15), run32(kk, 0), sub, run32(cb, 0), Op.is_le)
+        ts(q0("h2", 1, 30, 2), q0("tb", 16, 31), run32(kk, 2), sub, run32(cb, 2), Op.is_le)
+        fma(PO2, cb, 1.0, kk)
+        j = ts(WIN, run32(v2, 0), OWNV, Op.is_ge if grp else Op.is_gt)
+        for i in spread("oo", rg("xa", 143, 160, 16, 32, 64)):
+            if t < R - 1:
+                later(i, j)
+        pick("sl%d" % t, 128, "at", 0, G * A, rg("oo"))
+        scan(q0("kb", 32, 97), q0("hw", 0, 65), q0("h2", 0, 65), 0.0, mul, add)
+        fma(WC, WIN, 32.0, 64.0)
         fma(DCOL, WIN, 32.0, C0)
+        turn(q0("kt"), q0("kb", 64, 96))
+        ts(DM, KEY, float(N), Op.is_lt, DCOL, mul)
+        ts(q0("eq", 0, 32), q0("kt"), KEY, Op.is_equal, -1000.0, mul)
+        scan(q0("za"), q0("eq"), q0("da"), 1000.0 * (CAPP + 1), add, Op.min)
+        ts(N2, run32(PO2, 2), -BIG, add, run32(PO2, 0), Op.max)
+        ts(DN, N2, OWNN, sub, WIN, mul)
+        fma(FN, DN, 1.0, OWNN)
+        fma(T4, AN, -1.0, FN)
+
+    def candidates(t):
+        x0 = XW * t
         for b in range(4):
-            scp(rg("dl", b, 256, 4), rg("ps", 1024 + 512 * b, 1024 + 512 * b + 64))
-        turn(q0("kt"), q0("kb", 32, 64))
-        ts(q0("eq"), q0("kt"), KEY, Op.is_equal)
-        red(CNT, q0("eq"), add)
-
-    def step(t):
-        o, i, w, f = rg("xt", 128 * t + 128, 128 * t + 256), rg("xt", 128 * t, 128 * t + 128), rg("dl"), rg("of")
-        run("v", [o], [i, w, f], lambda: g.vector.tensor_tensor(ap(o), ap(w).indirect(ap(f)), ap(i), add))
-
-    def changed():
-        for c in range(2):
-            ts(q0("sm", 76 + c, 84, 2), q0("cs", 16 + c, 24, 2), q0("xa", 79 + 16 * c, 80 + 16 * c), Op.is_equal, q0("xd", 79 + 16 * c, 80 + 16 * c), mul)
+            mm(4 + b, "ep", 128 * b, "fa", 2 * M * (t + 1), 128, True, False)
+        for b in (2, 3, 0, 1):
+            mm(4 + b, "en", 128 * b, "sl%d" % t, 2 * M, 128, False, True)
+            tt(rg("xp", x0 + 128 * b + 64, x0 + 128 * b + 128), rg("ps", 512 * (4 + b) + 64, 512 * (4 + b) + 128), rg("xp", x0 + 128 * b, x0 + 128 * b + 64), add)
 
     def move(t):
-        ts(q0("xb", 0, 32), q0("mu"), CNT, Op.is_gt, WC, mul)
-        fold("xb", "k4")()
-        spread("of", q0("xb", 67, 96, 4), P4)
-        ts(DM, KEY, float(N), Op.is_lt, DCOL, mul)
-        ts(MISS, KEY, float(N), Op.is_lt)
-        step(t)
+        if t == R - 1:
+            ts(q0("xb", 0, 32), q0("mu"), ROOM, Op.is_lt, WC, mul)
+            turn(q0("xb", 32, 64), q0("xb", 0, 32))
+            for h in range(2):
+                summed(q0("xb", 72 + 16 * h, 88 + 16 * h), q0("xb", 32 + 16 * h, 48 + 16 * h), 1.0, (PL, PH)[h], sm(92 + h), Fn.Identity)
+            return
+        turn(q0("xb", 32, 64), q0("za", 32, 64))
+        for h in range(2):
+            scan(q0("xb", 66 + 17 * h, 83 + 17 * h), q0("ml", 17 * h, 17 * h + 17), q0("xb", 32 + 16 * h, 49 + 16 * h), HOLD, add, Op.max)
+        for a in range(4):
+            ts(rg("oe", 0, 2, 1, 32 * a, 32 * a + 32), q0("xb", 82, 100, 17), -HOLD, add)
+        f = rg("oe")
+        for b in (2, 3, 0, 1):
+            w, x1 = rg("xp", XW * t + 128 * b, XW * t + 128 * b + 128), XW * (t + 1) + 128 * b
+            gather(rg("xp", x1, x1 + 32), w, f)
+            if b < 2:
+                chosen(rg("et", b, 128, 4), w, f, rg("bt", b, 128, 4))
+            else:
+                tt(rg("et", b, 128, 4), rg("xp", x1, x1 + 32), rg("bt", b, 128, 4), add)
+            scp(rg("xp", x1 + 32, x1 + 64), rg("xp", x1, x1 + 32))
+        quant("es%d" % (t + 1), 160, 288, rg("et"))
+        send_e(t + 1)
 
     def slots(t):
-        ts(q0("xd", 0, 32), q0("mt"), CNT, Op.is_gt, DM, mul)
-        ts(FET, CNT, CAPP + 0.5, Op.is_lt, MISS, mul)
-        later = fold("xd", "k16")
-        ts(DN, q0("mi", 2 * t, 2 * t + 1), OWNN, sub, WIN, mul)
-        later()
-        ts(OF4, HOT, FET, mul)
-        changed()
-        ts(T4, AN, OWNN, sub, DN, sub)
+        ts(q0("xd", 0, 32), q0("mu"), ROOM, Op.is_lt, DM, mul)
+        turn(q0("xd", 32, 64), q0("xd", 0, 32))
+        scan(q0("xd", 64, 96), q0("k16"), q0("xd", 32, 64), 0.0, mul, add)
+        for c in range(2):
+            ts(q0("sm", 76 + c, 84, 2), q0("cs", 16 + c, 24, 2), q0("xa", 175 + 16 * c, 176 + 16 * c), Op.is_equal, q0("xd", 79 + 16 * c, 80 + 16 * c), mul)
         tt(L9, L8, BASEP, add)
+        spread("ol", L9 if t < R - 1 else sm(84, 10))
+        for b in range(4 * (t == R - 1)):
+            minus("sv"[b % 2], rg("pxs", b, 128, 4), rg("xp", XW * t + 128 * b, XW * t + 128 * b + 128), rg("ol", 8, 10))
+        ts(FET, ROOM, 500.0, Op.is_gt, DM, mul)
+        fma(OF4, HOT, FET, 0.0, Fn.Sign)
         tt(T5, T4, OF4, mul)
-        spread("ol", L9, 64.0)
-        tt(AN, AN, T5, sub)
-        pick("sl%d" % (t + 1), 64, "sl%d" % t, 0, 192, "ol")
-
-    def finish(t):
-        last = "sl%d" % R
-        ts(q0("xd", 0, 32), q0("mt"), CNT, Op.is_gt, DM, mul)
-        ts(q0("xb", 0, 32), q0("mu"), CNT, Op.is_gt, WC, mul)
-        sums = [fold("xd", "k16"), fold("xb", "k4")]
-        sums[0]()
-        sums[1]()
-        changed()
-        ts(DN, q0("mi", 2 * t, 2 * t + 1), OWNN, sub, WIN, mul)
-        tt(L9, L8, BASEP, add)
-        ts(FET, CNT, CAPP + 0.5, Op.is_lt, MISS, mul)
-        spread("ol", L9, 64.0)
-        ts(T4, AN, OWNN, sub, DN, sub)
-        pick(last, 64, "sl%d" % t, 0, 192, "ol")
-        store("y", T.oc[:, :], rg(last + "c", 64, 192), u8(rg(last + "c", 64, 192)))
-        spread("of", q0("xb", 67, 96, 4), P4)
-        ts(OF4, HOT, FET, mul)
-        products(t)
-        store("s", T.y[:, 256 * t:256 * t + 256], rg("ys", 256 * t, 256 * t + 256))
-        step(t)
-        tt(T5, T4, OF4, mul)
-        cp(rg("pxs"), rg("xt", 128 * R, 128 * R + 128))
-        tt(AN, AN, T5, sub)
-        for a in range(4):
-            store("y", T.osc[4 * a:4 * a + 4, :], rg(last + "s", 64, 192, 1, 32 * a, 32 * a + 4))
-        store("s", T.px[:, :], rg("pxs"))
-        turn(q0("ant"), q0("anb"))
-        store("y", T.an[:, :], rg("ant", 0, 32, 1, 0, 4))
+        tt(AN, AN, T5, add)
+        pick("sl%d" % (t + 1), 0, "sl%d" % t, 0, 192, rg("ol", 0, 8))
+        if t < R - 1:
+            table()
+        else:
+            products(t)
 
     for t in range(R):
         worst(t)
-        if t == 0:
-            quant("ep", 0, 512, rg("ct"))
-            wait("y", "set%d" % (near[0] % G), 2 * len(topo.engines(T.cores[near[0]], core)))
-            load("y", rg("wt"), T.w[:, :], "lw")
         score(t)
-        prepare(t)
-        if t:
-            wait("y", "cz%d" % t, ne)
-            store("y", T.y[:, 256 * (t - 1):256 * t], rg("ys", 256 * (t - 1), 256 * t))
-        else:
-            quant("wq", 0, 128 * O, rg("wt"))
         decide(t)
-        if t < R - 1:
-            move(t)
-            send_e(t + 1)
-            slots(t)
-        else:
-            ts(DM, KEY, float(N), Op.is_lt, DCOL, mul)
-            ts(MISS, KEY, float(N), Op.is_lt)
-            finish(t)
+        candidates(t)
+        move(t)
+        slots(t)
+    store("y", T.oc[:, :], rg("sl3c"), u8(rg("sl3c")), 2.1)
+    for a in range(4):
+        store("ys"[a % 2], T.osc[4 * a:4 * a + 4, :], rg("sl3s", 0, 128, 1, 32 * a, 32 * a + 4), lat=1.7)
+    store("y", T.px[:, :], rg("pxs"), lat=2.1)
+    fma(q0("anb", 0, 4), AN, 1.0, float(G * A * (1 - grp)))
+    turn(q0("ant"), q0("anb"))
+    store("y", T.an[:, :], rg("ant", 0, 32, 1, 0, 4), lat=1.7)
+
+    seen = {q: {} for q in Q}
+    count = {"vn": 0, "sn": 0, "tn": 0, "gn": 0, "sty": 0, "sts": 0}
+    for j in order(nodes):
+        n = nodes[j]
+        q = n["q"]
+        if q == "r":
+            n["knows"] = {n["sem"]: n["n"]}
+            continue
+        for d in sorted([d for d, w in n["deps"].items() if w], reverse=True):
+            m = nodes[d]
+            if seen[q].get(m["sem"], 0) < m["n"]:
+                n.setdefault("waits", {})[m["sem"]] = max(n.get("waits", {}).get(m["sem"], 0), m["n"])
+                for s, v in m["knows"].items():
+                    seen[q][s] = max(seen[q].get(s, 0), v)
+        for s, v in sorted(n.get("waits", {}).items()):
+            Q[q].wait_ge(T.sem[s], v)
+        made = n["call"]()
+        if n["sem"] is None:
+            n["sem"] = q + "n"
+            count[n["sem"]] += 1
+            n["n"] = count[n["sem"]]
+            made.then_inc(T.sem[n["sem"]], 1)
+        elif n["sem"] in count:
+            count[n["sem"]] += 16
+        n["knows"] = dict(seen[q])
+        n["knows"][n["sem"]] = n["n"]
     for q in "vstg":
-        wait("g", q + "n", count[q])
-    wait("g", "sent", count["sent"])
-    wait("y", "sty", count["sty"])
-    wait("s", "sts", count["sts"])
+        g.wait_ge(T.sem[q + "n"], count[q + "n"])
+    g.wait_ge(T.sem.sent, sent[0])
+    g.sync.wait_ge(T.sem.sty, count["sty"])
+    g.scalar.wait_ge(T.sem.sts, count["sts"])

from concourse.bass import DstId, RemoteDMATransfer
from concourse.mybir import dt, AluOpType, AxisListType, ActivationFunctionType

N, A, M, CAPP, R, O = 8, 320, 32, 3, 3, 2
CORES = 256
G = N // 2
PW = A // 2
BIG, HOLD = 1.0e6, 4096.0
XW = 512
CODE, F32, BF, I32, U8, U16 = "float8_e4m3fn_x4", "float32", "bfloat16", "int32", "uint8", "uint16"

SCRATCH = {}
for _n, _w in (("qd", A), ("at", G * A), ("rl", A), ("es0", 288), ("es1", 288), ("es2", 288), ("fa", 128 + 2 * M * R), ("ep", 512), ("en", 512),
               ("wq", 128 * O), ("ca", M * R), ("sl0", 192), ("sl1", 192), ("sl2", 192), ("sl3", 128)):
    SCRATCH[_n + "c"] = ("sbuf", [128, _w], CODE)
    SCRATCH[_n + "s"] = ("sbuf", [128, _w], U8)
for _n, _w, _d in (("dtile", 4 * A, BF), ("xt", 128, BF), ("xp", XW * R, BF), ("bt", 128, BF), ("wt", 512 * O, BF), ("et", 512, BF), ("zt", 512, BF),
                   ("ct", 2048, BF), ("rm", 2 * A, F32), ("sg", 2 * A, F32), ("ys", 768, F32), ("pxs", 128, F32),
                   ("idt", 128, BF), ("io1", 128, I32), ("io2", 32, I32), ("io3", 32, I32), ("ia", 32, I32), ("ib", 128, I32),
                   ("acti", 8, I32), ("mz", 32, F32), ("xe", 64, F32), ("mn", 32, F32), ("mu", 32, F32), ("k16", 32, F32),
                   ("dg", 128, F32), ("pen", 40, F32), ("cs", 48, F32), ("kb", 100, F32), ("hw", 72, F32), ("hv", 16, F32), ("kt", 32, F32),
                   ("eq", 64, F32), ("da", 64, F32), ("za", 64, F32), ("ml", 72, F32),
                   ("xa", 192, F32), ("xb", 112, F32), ("xd", 96, F32), ("sc", 384, F32), ("tb", 32, F32),
                   ("sm", 96, F32), ("h1", 16, F32), ("h2", 72, F32), ("anb", 32, F32), ("ant", 32, F32),
                   ("mo", 4 * R, F32), ("mi", 4 * R, F32), ("oa", 4, U16), ("oo", 2, U16), ("oe", 2, U16), ("ol", 10, U16)):
    SCRATCH[_n] = ("sbuf", [128, _w], _d)
SCRATCH["ps"] = ("psum", [128, 4096], F32)

SEMAPHORES = (["vn", "sn", "tn", "gn", "sent", "ld0", "ld1", "lx", "lb", "la", "la2", "lw", "sty", "sts", "rs", "rc"]
              + ["set%d" % k for k in range(G)]
              + ["%s%d" % (s, t) for s in ("ee", "me", "cc", "cz") for t in range(R)])


def bits(engines):
    m = 0
    for e in engines:
        m |= 1 << e
    return m


def partners(T, topo):
    free, out = list(range(G, N)), {}
    for r in range(G):
        q = [u for u in free if topo.may_write(T.cores[r], T.cores[u]) and topo.may_write(T.cores[u], T.cores[r])][0]
        free.remove(q)
        out[r], out[q] = q, r
    return out


def ways(T, topo, r):
    c = T.cores[r]
    group = [q for q in range(r // G * G, r // G * G + G) if q != r]
    near = [q for q in group if topo.may_write(c, T.cores[q])]
    far = [q for q in group if q not in near]
    home = [u for u in topo.cores_of(c) if topo.die(u) != topo.die(c) and all(topo.may_write(u, T.cores[q]) for q in far)]
    away = []
    for q in far:
        d = T.cores[q]
        able = [u for u in range(CORES) if topo.mates(u, d) and topo.may_write(u, d) and topo.may_write(c, u)]
        same = [u for u in able if topo.die(u) == topo.die(c)]
        other = [u for u in able if u not in same]
        away.append((same, other)[sorted([r] + near).index(r)][0])
    return near, far, [away, home[:2]]


def share(engines, n, j):
    w = len(engines) // n
    return engines[j * w:j * w + w]


def feed(T, topo, r, w, j):
    relays = ways(T, topo, r)[2]
    off = topo.engines(T.cores[r], relays[0][0])
    return share(off if w == 0 else [e for e in topo.engines(T.cores[r], relays[w][j]) if e not in off], 2, j)


def send(g, T, topo, core, moves):
    if len(moves) == 1:
        d, o, i, s, e = moves[0]
        rid, pid = topo.addr(d, core)
        g.remote_dma(o, i, T.sem[s], T.sem.sent, pid, rid, bits(e))
    else:
        ts = []
        for d, o, i, s, e in moves:
            rid, pid = topo.addr(d, core)
            ts.append(RemoteDMATransfer(dst_ids=[DstId(rid=rid, pnc=pid)], dma_engine_mask=bits(e), remote_sem=T.sem[s], src=i, dst=o))
        g.remote_dma_fused(ts, local_sem=T.sem.sent)
    return sum(len(m[4]) for m in moves)


def relay_program(g, core, T, topo, r, w, j):
    to = T.cores[ways(T, topo, r)[1][j]]
    c0, base, n = w * PW, (r % G) * A + w * PW, 0
    for x in "sc":
        src, dst = T["rl" + x][:, c0:c0 + PW], T["at" + x][:, base:base + PW]
        if x == "c":
            src, dst = src.bitcast(dt.uint8), dst.bitcast(dt.uint8)
        g.wait_ge(T.sem["r" + x], len(feed(T, topo, r, w, j)))
        n += send(g, T, topo, core, [(to, dst, src, "set%d" % (r % G), topo.engines(core, to))])
    g.wait_ge(T.sem.sent, n)


CYC, WAKE = 1.04e-3, 0.09


def order(nodes):
    after = [[] for _ in nodes]
    for j, n in enumerate(nodes):
        for i in n["deps"]:
            after[i].append(j)
    left = [0.0] * len(nodes)
    for i in range(len(nodes) - 1, -1, -1):
        left[i] = max([nodes[i]["lat"]] + [left[j] + (nodes[i]["lat"] + WAKE if nodes[j]["deps"][i] else nodes[i]["hold"]) for j in after[i]])
    miss = [len(n["deps"]) for n in nodes]
    ready = [i for i in range(len(nodes)) if not miss[i]]
    done, free, out, end = {}, {}, [], max(left)
    while ready:
        est = {}
        for i in ready:
            n = nodes[i]
            est[i] = max([free.get(n["q"], 0.0) if n["q"] != "r" else 0.0] + [done[d][0] + WAKE if w else done[d][1] for d, w in n["deps"].items()])
        first = min(ready, key=lambda i: (est[i], -left[i]))
        q = nodes[first]["q"]
        mine = [i for i in ready if nodes[i]["q"] == q]
        pick = max([i for i in mine if est[i] <= est[first] + 0.02], key=lambda i: left[i])
        if q != "r":
            stop = est[pick] + nodes[pick]["hold"]
            urgent = [i for i in mine if left[i] > left[pick] and est[i] < stop and stop + left[i] > end - 1.0]
            if urgent:
                pick = min(urgent, key=lambda i: (est[i], -left[i]))
        n = nodes[pick]
        free[q] = est[pick] + n["hold"]
        done[pick] = (est[pick] + n["lat"], est[pick])
        end = max(end, est[pick] + left[pick])
        ready.remove(pick)
        out.append(pick)
        for j in after[pick]:
            miss[j] -= 1
            if not miss[j]:
                ready.append(j)
    return out


def rank_program(g, core, T, topo):
    rank = T.rank_of(core)
    if rank is None:
        for r in range(N):
            for w, row in enumerate(ways(T, topo, r)[2]):
                if core in row:
                    relay_program(g, core, T, topo, r, w, row.index(core))
        return
    k, grp = rank % G, rank // G
    near, far, relays = ways(T, topo, rank)
    mate = T.cores[partners(T, topo)[rank]]
    em = topo.engines(core, mate)
    ne = len(topo.engines(mate, core))
    Q = {"v": g.vector, "s": g.scalar, "t": g.tensor, "g": g, "y": g.sync}
    nodes, log, last = [], {}, {}
    sent = [0]
    add, sub, mul, Op, Fn = AluOpType.add, AluOpType.subtract, AluOpType.mult, AluOpType, ActivationFunctionType

    def rg(name, c0=0, c1=None, step=1, p0=0, p1=128):
        return (name, p0, p1, c0, SCRATCH[name][1][1] if c1 is None else c1, step)

    def q0(name, c0=0, c1=None, step=1):
        return rg(name, c0, c1, step, 0, 32)

    def h0(name, c0=0, c1=None, step=1):
        return rg(name, c0, c1, step, 0, 64)

    def half(r, h):
        return r[:1] + (64 * h, 64 * h + 64) + r[3:]

    def run32(r, a):
        return r[:1] + (32 * a, 32 * a + 32) + r[3:]

    def ap(r):
        if not isinstance(r, tuple):
            return r
        return T[r[0]][r[1]:r[2], r[3]:r[4]:r[5]] if r[5] != 1 else T[r[0]][r[1]:r[2], r[3]:r[4]]

    def wide(r):
        return len(range(r[3], r[4], r[5]))

    def meet(a, b):
        if a[0] == "ps":
            return a[3] // 512 == b[3] // 512
        if a[1] >= b[2] or b[1] >= a[2] or a[3] >= b[4] or b[3] >= a[4]:
            return False
        return not (a[5] == b[5] and (a[3] - b[3]) % a[5])

    def node(q, outs, ins, call, hold, lat=None, sem=None, n=0, behind=(), chain=None):
        deps = {}
        uses = [(r, True) for r in outs] + [(r, False) for r in ins if isinstance(r, tuple)]
        for r, w in uses:
            for r2, w2, j in log.get(r[0], ()):
                if meet(r, r2):
                    if r[0] == "ps":
                        if nodes[j]["q"] != q:
                            deps[j] = True
                        elif q == "t":
                            deps.setdefault(j, False)
                    elif w or w2:
                        deps[j] = True
        for j in behind:
            deps[j] = True
        if chain:
            if chain in last:
                deps.setdefault(last[chain], False)
            last[chain] = len(nodes)
        for r, w in uses:
            log.setdefault(r[0], []).append((r, w, len(nodes)))
        nodes.append({"q": q, "deps": deps, "call": call, "hold": hold, "lat": hold if lat is None else lat, "sem": sem, "n": n})
        return len(nodes) - 1

    def later(j, d):
        nodes[j]["deps"].setdefault(d, False)

    def run(q, outs, ins, call, cyc=64):
        return node(q, outs, ins, call, max(64, cyc) * CYC, chain="g" if q == "g" else None)

    def load(q, out, src, sem, lat, behind=()):
        return node(q, [out], [], lambda: Q[q].dma_start(ap(out), src).then_inc(T.sem[sem], 16), 0.06, lat, sem, 16, behind, "load" + q)

    def store(q, dst, src, view=None, lat=2.0, behind=()):
        node(q, [], [src], lambda: Q[q].dma_start(dst, view if view is not None else ap(src)).then_inc(T.sem["st" + q], 16), 0.06, lat, "st" + q, 0, behind)

    def post(srcs, moves):
        def call():
            sent[0] += send(g, T, topo, core, moves)
        return node("g", [], srcs, call, 0.12, 0.12, "sent", 0, (), "g")

    def lands(outs, sem, n, mirror, lat):
        j = node("r", outs, [], None, lat, lat, sem, n)
        later(j, mirror)
        return j

    def u8(r):
        return ap(r).bitcast(dt.uint8)

    def view(r):
        return u8(r) if SCRATCH[r[0]][2] == CODE else ap(r)

    def ts(o, i, s1, op0, s2=None, op1=None):
        if op1 is None:
            return run("v", [o], [i, s1], lambda: g.vector.tensor_scalar(ap(o), ap(i), ap(s1), None, op0), wide(o))
        return run("v", [o], [i, s1, s2], lambda: g.vector.tensor_scalar(ap(o), ap(i), ap(s1), ap(s2), op0, op1), wide(o))

    def tt(o, a, b, op):
        run("v", [o], [a, b], lambda: g.vector.tensor_tensor(ap(o), ap(a), ap(b), op), wide(o) * (1 if a[0] == "ps" else 2))

    def scan(o, a, b, first, op0, op1):
        run("v", [o], [a, b, first], lambda: g.vector.tensor_tensor_scan(ap(o), ap(a), ap(b), ap(first), op0, op1), wide(o))

    def cp(o, i):
        return run("v", [o], [i], lambda: g.vector.tensor_copy(ap(o), ap(i)), wide(o))

    def scp(o, i):
        run("s", [o], [i], lambda: g.scalar.activation(ap(o), ap(i), Fn.Copy), wide(o))

    def fma(o, i, scale, bias, fn=Fn.Identity):
        run("s", [o], [i, scale, bias], lambda: g.scalar.activation(ap(o), ap(i), fn, bias=ap(bias), scale=ap(scale)), wide(o))

    def summed(o, i, scale, bias, n, fn):
        run("s", [o, n], [i, bias], lambda: g.scalar.activation(ap(o), ap(i), fn, bias=ap(bias), scale=scale, accum_out=ap(n)), max(64, wide(o)) + 24)

    def ahead(o, i, n):
        summed(o, i, -1.0, i[:3] + (i[4] - 1, i[4], 1), n, Fn.Sign)

    def fill(o, v):
        run("v", [o], [], lambda: g.vector.memset(ap(o), v), wide(o) // (2 if SCRATCH[o[0]][2] == BF else 1))

    def turn(o, i):
        run("v", [o], [i], lambda: g.vector.transpose(ap(o), ap(i)), wide(o))

    def quant(name, c0, c1, i):
        c, s = rg(name + "c", c0, c1), rg(name + "s", c0, c1)
        return run("v", [c, s], [i], lambda: g.vector.quantize_mx(ap(c), ap(s), ap(i)), 15 + 1.06 * (c1 - c0))

    def mm(bank, st, s0, mv, m0, n, start, stop):
        o = rg("ps", 512 * bank, 512 * bank + n)
        i = [rg(st + "c", s0, s0 + 128), rg(st + "s", s0, s0 + 128), rg(mv + "c", m0, m0 + n), rg(mv + "s", m0, m0 + n)]
        return run("t", [o], i, lambda: g.tensor.matmul_mx(ap(o), ap(i[0]), ap(i[1]), ap(i[2]), ap(i[3]), start, stop), 0.6 * (n + 16))

    def gather(o, i, f):
        run("s", [o], [i, f], lambda: g.scalar.activation(ap(o), ap(i).indirect(ap(f)), Fn.Copy), 78 + 1.5 * wide(o))

    def chosen(o, i, f, b):
        run("v", [o], [i, f, b], lambda: g.vector.tensor_tensor(ap(o), ap(i).indirect(ap(f)), ap(b), add), 60 + 1.5 * wide(o))

    def minus(q, o, i, f):
        if q == "v":
            run("v", [o], [i, f], lambda: g.vector.tensor_scalar(ap(o), ap(i).indirect(ap(f)), -1.0, None, mul), 60 + 1.5 * wide(o))
        else:
            run("s", [o], [i, f], lambda: g.scalar.activation(ap(o), ap(i).indirect(ap(f)), Fn.Identity, bias=0.0, scale=-1.0), 78 + 1.5 * wide(o))

    def pick(dst, d0, src, s0, s1, f):
        n = 16 * wide(f)
        o, i = rg(dst + "c", d0, d0 + n), rg(src + "c", s0, s1)
        run("v", [o], [i, f], lambda: g.vector.tensor_copy(ap(o).bitcast(dt.uint32), ap(i).bitcast(dt.uint32).indirect(ap(f))), 60 + 1.5 * n)
        gather(rg(dst + "s", d0, d0 + n), rg(src + "s", s0, s1), f)

    def spread(off, src):
        return [cp(rg(off, 0, wide(src), 1, 32 * a, 32 * a + 32), src) for a in range(4)]

    load("y", rg("dtile", 0, 4 * PW), T.d[:, 0:4 * PW], "ld0", 0.5)
    load("y", rg("dtile", 4 * PW, 4 * A), T.d[:, 4 * PW:4 * A], "ld1", 0.8)
    load("y", rg("xt"), T.x[:, :], "lx", 1.0)
    load("y", rg("bt"), T.b[:, :], "lb", 1.1)
    load("s", rg("acti", p0=0, p1=16), T.act[:, :], "la", 2.0)
    load("s", rg("acti", p0=16, p1=32), T.act[:, :], "la2", 2.2)
    run("g", [rg("io1")], [], lambda: g.iota(T.io1[:], [[-1, 128]], 128, 1), 330)
    run("g", [rg("io2")], [], lambda: g.iota(T.io2[:], [[0, 2], [1, 16]], 0, 0), 180)
    run("g", [rg("io3")], [], lambda: g.iota(T.io3[:], [[1, 32]], 0, 0), 180)

    for w in range(2):
        quant("qd", w * PW, w * PW + PW, rg("dtile", 4 * PW * w, 4 * PW * w + 4 * PW))
        for x in "sc":
            src = rg("qd" + x, w * PW, w * PW + PW)
            relayed = post([src], [(u, view(rg("rl" + x, w * PW, w * PW + PW)), view(src), "r" + x, feed(T, topo, rank, w, j)) for j, u in enumerate(relays[w])])
    for x in "cs":
        src = rg("qd" + x)
        direct = post([src], [(T.cores[q], view(rg("at" + x, k * A, k * A + A)), view(src), "set%d" % k, topo.engines(core, T.cores[q])) for q in near])

    def send_e(t, lat=1.3):
        for x in "cs":
            src = rg("es%d%s" % (t, x), 160, 192)
            j = post([src], [(mate, view(rg("es%d%s" % (t, x), 128, 160)), view(src), "ee%d" % t, em)])
        lands([rg("es%dc" % t, 128, 160), rg("es%ds" % t, 128, 160)], "ee%d" % t, 2 * ne, j, lat)

    fill(rg("zt"), 0.0)
    scp(rg("et", 128, 512), rg("zt", 0, 384))
    tt(rg("et", 0, 128), rg("bt"), rg("xt"), sub)
    quant("es0", 160, 288, rg("et"))
    send_e(0, 6.8)
    for q in range(grp * G, grp * G + G):
        if q != rank:
            qn, qf, qr = ways(T, topo, q)
            j = q % G
            outs = [rg("atc", j * A, j * A + A), rg("ats", j * A, j * A + A)]
            if rank in qn:
                got = lands(outs, "set%d" % j, 2 * len(topo.engines(T.cores[q], core)), direct, 7.3)
            else:
                lands(outs, "set%d" % j, sum(2 * len(topo.engines(row[qf.index(rank)], core)) for row in qr), relayed, 8.0)
    load("y", rg("wt"), T.w[:, :], "lw", 2.6, [got])

    def cs(c, n=1, rows=q0):
        return rows("cs", c, c + n)

    def sm(c, n=1, rows=q0):
        return rows("sm", c, c + n)

    NEG4, BASEP, HI, PM, PH, PI, PP, PL = cs(8, 4), cs(16, 8), cs(24), cs(25), cs(26), cs(27), cs(28), cs(29)
    P128 = q0("io1", 0, 1)
    own0 = float((2 * grp - 1) * G * A)
    quant("at", k * A, k * A + A, rg("dtile"))
    for t in range(R):
        quant("es%d" % t, 0, 128, rg("zt"))
    quant("fa", 0, 128, rg("zt"))
    for b in range(4):
        for c in range(2):
            fma(rg("xp", 128 * b + 32 * c, 128 * b + 32 * c + 32), rg("xt", b, 128, 4), -1.0, 0.0)
    ts(rg("idt"), rg("io1"), 128.0, Op.is_equal)
    for b in range(4):
        scp(rg("ct", 512 * b, 512 * b + 512), rg("zt"))
    for name, v in (("ep", 0.25), ("en", -0.25)):
        for b in range(4):
            fma(rg("ct", 512 * b + b, 512 * b + 512, 4), rg("idt"), v, 0.0)
        for b in range(0, 4, 2):
            quant(name, 128 * b, 128 * b + 256, rg("ct", 512 * b, 512 * b + 1024))
    fill(rg("mo"), 0.0)
    fill(q0("anb"), 0.0)
    ts(rg("ia"), rg("io1", 0, 32), 15, Op.bitwise_and)
    ts(q0("ib"), q0("io1"), 31, Op.bitwise_and)
    ts(q0("pen", 0, 33), q0("io1", 0, 33), 128.0, Op.is_gt, 1000.0, mul)
    fill(q0("hw"), 1.0)
    fill(q0("hw", 0, 16, 2), -1.0)
    ts(q0("hw", 16, 17), P128, 8.0, mul, 16.0 - 8 * 128, add)
    cp(q0("hv", 0, 15), q0("hw", 0, 30, 2))
    ts(HI, P128, 128.0 + 16, Op.is_ge)
    cp(PI, P128)
    ts(PP, P128, -128.0, add)
    ts(q0("tb", 8, 15), q0("io3", 0, 7), float(A), mul, float(A - G * A * (1 - grp)), add)
    ts(rg("mz"), rg("ia"), 0.0, Op.is_gt, -BIG, mul)
    ts(q0("mn"), q0("ia"), 0.0, Op.is_equal, -1.0, mul)
    ts(q0("mu"), q0("mz"), -1.0, mul, 500.0, add)
    ts(q0("dg"), q0("ib"), 0.0, Op.is_gt, 1.0e29, mul)
    ts(q0("k16"), q0("io2"), 0.0, Op.is_gt)
    cp(PM, q0("ia", 0, 1))
    ts(PH, q0("ia", 0, 1), 16.0, add, 1.0 / 16, mul)
    ts(PL, q0("ia", 0, 1), 1.0 / 16, mul)
    fill(q0("eq", 32, 64), 0.0)
    fill(q0("da"), BIG)
    fill(q0("xb", 64, 65), 0.0)
    ts(q0("ml", 36, 53), q0("io3", 0, 17), PM, Op.is_equal, -HOLD, mul)
    ts(q0("ml", 54, 71), q0("io3", 0, 17), -1.0, add, PM, Op.is_equal)
    for h in range(2):
        ts(sm(10 + h), PM, HOLD + 16 * h, add)
        ts(q0("ml", 17 * h, 17 * h + 17), q0("ml", 54, 71), sm(10 + h), mul)
        tt(q0("ml", 17 * h, 17 * h + 17), q0("ml", 17 * h, 17 * h + 17), q0("ml", 36, 53), add)
    ts(BASEP, q0("io3", 0, 8), 16.0, mul, PM, add)
    ts(NEG4, q0("io3", 0, 4), -32.0, mul, PP, sub)
    cp(q0("h2", 32, 33), q0("pen", 0, 1))
    tt(q0("h2", 33, 65), q0("pen", 1, 33), q0("pen", 0, 32), sub)
    ts(half(rg("mz"), 1), half(rg("mz"), 1), -BIG, add)

    AN, AN1 = q0("tb", 1, 8, 2), q0("tb", 0, 8, 2)

    def table():
        fma(AN1, AN, 1.0, 1.0)
        fma(q0("tb", 16, 31), q0("tb", 0, 15), 1.0, BIG)

    spread("ol", q0("acti"))
    pick("sl0", 0, "at", k * A, k * A + A, rg("ol", 0, 8))
    tt(sm(0, 4), q0("acti", 1, 8, 2), q0("acti", 0, 8, 2), sub)
    ts(sm(4, 4), sm(0, 4), HI, mul, A * k + own0, add)
    tt(AN, sm(4, 4), q0("acti", 0, 8, 2), add)
    table()

    NPOS, HOT, C0 = sm(20), sm(21, 4), sm(25)
    CA, POS, K2, PO2, FC = [sm(c, 1, rg) for c in range(26, 31)]
    OWNN, OWNV, N1, N2, DCOL, DM = sm(46), sm(47), sm(48), sm(49), sm(52), sm(54)
    ROOM, WC = q0("za", 31, 32), q0("da", 32, 33)
    DN, FN, FET, OF4, T4, T5, L8, L9 = sm(60), sm(61), sm(62), sm(64, 4), sm(68, 4), sm(72, 4), sm(76, 8), sm(84, 8)
    KEY, NKEY, KEY1, WIN = q0("kb", 96, 97), q0("h2", 30, 31), q0("h2", 31, 32), q0("hw", 31, 32)

    def worst(t):
        mm(6, "es%d" % t, 160, "sl%d" % t, 0, 128, True, True)
        tt(q0("sc", 0, 128), q0("ps", 3072, 3200), q0("dg"), add)
        scan(q0("sc", 128, 256), q0("sc", 0, 128), q0("sc", 0, 128), 5.0e29, Op.min, Op.min)
        ahead(q0("sc", 256, 384), q0("sc", 128, 256), NPOS)
        fma(C0, NPOS, 1.0, PI)
        fma(q0("xe", 0, 32), q0("mn"), NPOS, 0.0)
        turn(q0("xe", 32, 64), q0("xe", 0, 32))
        scan(q0("xa", 160, 192), q0("k16"), q0("xe", 32, 64), 0.0, mul, add)
        ts(HOT, NEG4, NPOS, Op.is_equal)

    def products(t, behind=()):
        for o in range(O):
            j = mm(2 + o, "wq", 128 * o, "sl%d" % (t + 1), 0, 128, True, True)
            if behind:
                later(j, behind[0])
            (cp if o and t == R - 1 else scp)(rg("ys", 256 * t + 128 * o, 256 * t + 128 * o + 128), rg("ps", 512 * (2 + o), 512 * (2 + o) + 128))
        store("y", T.y[:, 256 * t:256 * t + 256], rg("ys", 256 * t, 256 * t + 256), lat=2.3, behind=behind[1:])

    def score(t):
        es = "es%d" % t
        CB, KK = rg("mo", 4 * t, 4 * t + 1), rg("mo", 4 * t + 2, 4 * t + 3)
        L0, L1 = rg("rm", A - 1, A), rg("rm", 2 * A - 1, 2 * A)
        lo, hi = half(L1, 0), half(L1, 1)
        for c in range(2):
            mm(c, es, 128, "at", c * A, A, True, False)
            mm(c, es, 64, "at", (2 + c) * A, A, False, True)
            o = rg("rm", c * A, c * A + A)
            scan(o, rg("ps", 512 * c, 512 * c + A), rg("zt", 0, A), L0 if c else -1.0e29, Op.max, add)
            ahead(rg("sg", c * A, c * A + A), o, (CA, CB)[c])
        top = h0("mo", 4 * t + 1, 4 * t + 2)
        ts(half(FC, 0), hi, lo, Op.is_gt, -BIG, mul)
        ts(half(FC, 1), hi, lo, Op.is_gt, BIG + 2 * A, mul)
        ts(K2, L0, L1, Op.is_lt, float(A), mul)
        ts(KK, K2, CA, Op.max, FC, add)
        ts(top, hi, lo, Op.max)
        for h in range(2):
            ts(h0("xa", 32 * h, 32 * h + 32), half(rg("mz"), h), half(KK, h), add, half(CB, h), add)
        fma(POS, CB, 1.0, KK)
        src = rg("mo", 4 * t, 4 * t + 3)
        j = post([src], [(mate, ap(rg("mi", 4 * t, 4 * t + 3)), ap(src), "me%d" % t, em)])
        lands([rg("mi", 4 * t, 4 * t + 3)], "me%d" % t, ne, j, 1.8)
        turn(h0("xa", 64, 128), h0("xa", 0, 64))
        for h in range(2):
            scan(h0("xa", 128 + 16 * h, 144 + 16 * h), h0("xa", 64 + 16 * h, 80 + 16 * h), h0("xa", 96 + 16 * h, 112 + 16 * h), 0.0, Op.max, Op.max)
        spread("oa", q0("xa", 143, 192, 16))
        pick("ca", M * t, "at", 0, G * A, rg("oa", 0, 2))
        for x, sem, lat in (("c", "cc", 1.6), ("s", "cz", 1.8)):
            src, dst = rg("ca" + x, M * t, M * t + M), rg("sl%d%s" % (t, x), 160, 192)
            j = post([src], [(mate, view(dst), view(src), "%s%d" % (sem, t), em)])
            came = lands([dst], "%s%d" % (sem, t), ne, j, lat)
        if t:
            products(t - 1, [j, came])
        else:
            later(quant("wq", 0, 128 * O, rg("wt")), j)
        ts(N1, run32(POS, 3), -BIG, add, run32(POS, 1), Op.max)
        fma(OWNN, N1, 1.0, own0)
        cp(OWNV, run32(top, 1))
        ts(q0("h1", 0, 15), q0("tb", 0, 15), OWNN, Op.is_le)
        scan(q0("h2", 17, 32), q0("hv", 0, 15), q0("h1", 0, 15), 0.0, mul, add)
        fma(NKEY, KEY1, -1.0, 0.0)
        for c in range(2):
            pick("fa", 128 + M * (2 * t + c), "sl%d" % t, 0, 128, rg("oa", 2, 4))

    def decide(t):
        cb, v2, kk = [rg("mi", 4 * t + c, 4 * t + c + 1) for c in range(3)]
        ts(q0("h2", 0, 30, 2), q0("tb", 0, 15), run32(kk, 0), sub, run32(cb, 0), Op.is_le)
        ts(q0("h2", 1, 30, 2), q0("tb", 16, 31), run32(kk, 2), sub, run32(cb, 2), Op.is_le)
        fma(PO2, cb, 1.0, kk)
        j = ts(WIN, run32(v2, 0), OWNV, Op.is_ge if grp else Op.is_gt)
        for i in spread("oo", rg("xa", 143, 160, 16, 32, 64)):
            if t < R - 1:
                later(i, j)
        pick("sl%d" % t, 128, "at", 0, G * A, rg("oo"))
        scan(q0("kb", 32, 97), q0("hw", 0, 65), q0("h2", 0, 65), 0.0, mul, add)
        fma(WC, WIN, 32.0, 64.0)
        fma(DCOL, WIN, 32.0, C0)
        turn(q0("kt"), q0("kb", 64, 96))
        ts(DM, KEY, float(N), Op.is_lt, DCOL, mul)
        ts(q0("eq", 0, 32), q0("kt"), KEY, Op.is_equal, -1000.0, mul)
        scan(q0("za"), q0("eq"), q0("da"), 1000.0 * (CAPP + 1), add, Op.min)
        ts(N2, run32(PO2, 2), -BIG, add, run32(PO2, 0), Op.max)
        ts(DN, N2, OWNN, sub, WIN, mul)
        fma(FN, DN, 1.0, OWNN)
        fma(T4, AN, -1.0, FN)

    def candidates(t):
        x0 = XW * t
        for b in range(4):
            mm(4 + b, "ep", 128 * b, "fa", 2 * M * (t + 1), 128, True, False)
        for b in (2, 3, 0, 1):
            mm(4 + b, "en", 128 * b, "sl%d" % t, 2 * M, 128, False, True)
            tt(rg("xp", x0 + 128 * b + 64, x0 + 128 * b + 128), rg("ps", 512 * (4 + b) + 64, 512 * (4 + b) + 128), rg("xp", x0 + 128 * b, x0 + 128 * b + 64), add)

    def move(t):
        if t == R - 1:
            ts(q0("xb", 0, 32), q0("mu"), ROOM, Op.is_lt, WC, mul)
            turn(q0("xb", 32, 64), q0("xb", 0, 32))
            for h in range(2):
                summed(q0("xb", 72 + 16 * h, 88 + 16 * h), q0("xb", 32 + 16 * h, 48 + 16 * h), 1.0, (PL, PH)[h], sm(92 + h), Fn.Identity)
            return
        turn(q0("xb", 32, 64), q0("za", 32, 64))
        for h in range(2):
            scan(q0("xb", 66 + 17 * h, 83 + 17 * h), q0("ml", 17 * h, 17 * h + 17), q0("xb", 32 + 16 * h, 49 + 16 * h), HOLD, add, Op.max)
        for a in range(4):
            ts(rg("oe", 0, 2, 1, 32 * a, 32 * a + 32), q0("xb", 82, 100, 17), -HOLD, add)
        f = rg("oe")
        for b in (2, 3, 0, 1):
            w, x1 = rg("xp", XW * t + 128 * b, XW * t + 128 * b + 128), XW * (t + 1) + 128 * b
            gather(rg("xp", x1, x1 + 32), w, f)
            if b < 2:
                chosen(rg("et", b, 128, 4), w, f, rg("bt", b, 128, 4))
            else:
                tt(rg("et", b, 128, 4), rg("xp", x1, x1 + 32), rg("bt", b, 128, 4), add)
            scp(rg("xp", x1 + 32, x1 + 64), rg("xp", x1, x1 + 32))
        quant("es%d" % (t + 1), 160, 288, rg("et"))
        send_e(t + 1)

    def slots(t):
        ts(q0("xd", 0, 32), q0("mu"), ROOM, Op.is_lt, DM, mul)
        turn(q0("xd", 32, 64), q0("xd", 0, 32))
        scan(q0("xd", 64, 96), q0("k16"), q0("xd", 32, 64), 0.0, mul, add)
        for c in range(2):
            ts(q0("sm", 76 + c, 84, 2), q0("cs", 16 + c, 24, 2), q0("xa", 175 + 16 * c, 176 + 16 * c), Op.is_equal, q0("xd", 79 + 16 * c, 80 + 16 * c), mul)
        tt(L9, L8, BASEP, add)
        spread("ol", L9 if t < R - 1 else sm(84, 10))
        for b in range(4 * (t == R - 1)):
            minus("sv"[b % 2], rg("pxs", b, 128, 4), rg("xp", XW * t + 128 * b, XW * t + 128 * b + 128), rg("ol", 8, 10))
        ts(FET, ROOM, 500.0, Op.is_gt, DM, mul)
        fma(OF4, HOT, FET, 0.0, Fn.Sign)
        tt(T5, T4, OF4, mul)
        tt(AN, AN, T5, add)
        pick("sl%d" % (t + 1), 0, "sl%d" % t, 0, 192, rg("ol", 0, 8))
        if t < R - 1:
            table()
        else:
            products(t)

    for t in range(R):
        worst(t)
        score(t)
        decide(t)
        candidates(t)
        move(t)
        slots(t)
    store("y", T.oc[:, :], rg("sl3c"), u8(rg("sl3c")), 2.1)
    for a in range(4):
        store("ys"[a % 2], T.osc[4 * a:4 * a + 4, :], rg("sl3s", 0, 128, 1, 32 * a, 32 * a + 4), lat=1.7)
    store("y", T.px[:, :], rg("pxs"), lat=2.1)
    fma(q0("anb", 0, 4), AN, 1.0, float(G * A * (1 - grp)))
    turn(q0("ant"), q0("anb"))
    store("y", T.an[:, :], rg("ant", 0, 32, 1, 0, 4), lat=1.7)

    seen = {q: {} for q in Q}
    count = {"vn": 0, "sn": 0, "tn": 0, "gn": 0, "sty": 0, "sts": 0}
    for j in order(nodes):
        n = nodes[j]
        q = n["q"]
        if q == "r":
            n["knows"] = {n["sem"]: n["n"]}
            continue
        for d in sorted([d for d, w in n["deps"].items() if w], reverse=True):
            m = nodes[d]
            if seen[q].get(m["sem"], 0) < m["n"]:
                n.setdefault("waits", {})[m["sem"]] = max(n.get("waits", {}).get(m["sem"], 0), m["n"])
                for s, v in m["knows"].items():
                    seen[q][s] = max(seen[q].get(s, 0), v)
        for s, v in sorted(n.get("waits", {}).items()):
            Q[q].wait_ge(T.sem[s], v)
        made = n["call"]()
        if n["sem"] is None:
            n["sem"] = q + "n"
            count[n["sem"]] += 1
            n["n"] = count[n["sem"]]
            made.then_inc(T.sem[n["sem"]], 1)
        elif n["sem"] in count:
            count[n["sem"]] += 16
        n["knows"] = dict(seen[q])
        n["knows"][n["sem"]] = n["n"]
    for q in "vstg":
        g.wait_ge(T.sem[q + "n"], count[q + "n"])
    g.wait_ge(T.sem.sent, sent[0])
    g.sync.wait_ge(T.sem.sty, count["sty"])
    g.scalar.wait_ge(T.sem.sts, count["sts"])
